import numpy as np
import ml_dtypes


def mxq(x, axis, fmt="e4m3"):
    dtype, down = {"e4m3": (ml_dtypes.float8_e4m3fn, 7), "e5m2": (ml_dtypes.float8_e5m2, 14)}[fmt]
    v = np.moveaxis(np.asarray(x, np.float32).astype(ml_dtypes.bfloat16).astype(np.float64), axis, -1)
    blocks = v.reshape(v.shape[:-1] + (-1, 32))
    amax = np.abs(blocks).max(-1, keepdims=True)
    byte = np.maximum(np.where(amax > 0, np.frexp(amax)[1] - 1 + 127, 0) - down, 1)
    scale = np.exp2(byte - 127.0)
    codes = (blocks / scale).astype(np.float32).astype(dtype).astype(np.float64)
    return np.moveaxis((codes * scale).reshape(v.shape), -1, axis)


WIDE = False


def mx_kscale(k):
    if not WIDE:
        return np.ones(k)
    levels = np.array([10, -10, 5, -5, 0])
    if k % 512:
        return np.exp2(np.random.permutation(np.resize(levels, k // 32))).repeat(32)
    a = np.empty((k // 512, 16))
    for p in range(k // 512):
        a[p, :8] = np.random.permutation(np.resize(levels, 8))
        for g in range(8):
            far = levels[np.abs(levels - a[p, g]) >= 10]
            a[p, g + 8] = far[np.random.randint(len(far))]
    return np.exp2(a.ravel()).repeat(32)


def f64(x):
    return np.asarray(x).astype(np.float64)


def striped(idx):
    return np.tile(idx.reshape(-1, 16).T, (8, 1)).astype(np.uint16)


def unstriped(offs):
    return offs[:16].T.reshape(-1).astype(np.int64)


def pack_weight(w):
    k, n = w.shape
    w = f64(np.asarray(w, np.float32).astype(ml_dtypes.bfloat16)).reshape(k // 32, 32, n)
    amax = np.abs(w).max(1)
    byte = np.clip(np.where(amax > 0, np.frexp(amax)[1] - 1 + 127 - 7, 1), 1, 254)
    scaled = (w * np.exp2(127.0 - byte)[:, None, :]).reshape(k, n).astype(np.float32)
    words = np.ascontiguousarray(scaled.reshape(k // 512, 128, 4, n).transpose(0, 1, 3, 2)).astype(ml_dtypes.float8_e4m3fn).view(np.uint8)
    return words, np.ascontiguousarray(byte.astype(np.uint8).reshape(k // 512, 16, n))


def unpack_weight(words, scales):
    g, p, n, _ = words.shape
    vals = np.ascontiguousarray(words).view(ml_dtypes.float8_e4m3fn).astype(np.float64) * np.repeat(np.exp2(scales.astype(np.float64) - 127.0), 8, axis=1)[..., None]
    return vals.transpose(0, 1, 3, 2).reshape(g * 512, n)


K, T, S, N, R = 1024, 2048, 512, 256, 256


def setup_inputs():
    n = np.random.standard_normal
    s = mx_kscale(K)[:, None]
    c = mx_kscale(S)
    packed_xT = pack_weight(n((K, T)) * s)
    return {
        "x_words": packed_xT[0],
        "x_scales": packed_xT[1],
        "cT": (n((K, N)) / np.sqrt(K) / s).astype(np.float32),
        "area": (np.random.uniform(0.5, 1.0, (S, 1)) * c[:, None]).astype(np.float32),
        "qm": (n((S, R)) / np.sqrt(S) / c[:, None]).astype(np.float32),
        "cur": (n((R, N))).astype(np.float32),
        "offs": striped(np.random.permutation(T)[:S]),
        "right": striped(np.random.permutation(T)[:S]),
    }


def reference(x_words, x_scales, cT, area, qm, cur, offs, right):
    xq = unpack_weight(x_words, x_scales)[:, unstriped(offs)]
    cTq = mxq(f64(cT), 0, "e4m3")
    lt = xq.T @ cTq
    x_right = unpack_weight(x_words, x_scales)[:, unstriped(right)]
    rt = x_right.T @ cTq
    a = np.maximum(np.abs(lt), np.abs(rt))
    jump = rt - lt
    flux = 0.25 * ((lt) ** 2 + (rt) ** 2) - (0.5 * (a * jump))
    fa = f64(area) * flux
    return f64(cur) - (0.5 * ((mxq(f64(qm), 0, "e4m3").T @ mxq(fa, 0, "e4m3"))))

@@ -1,0 +1,183 @@
+from contextlib import ExitStack
+
+import concourse.mybir as mybir
+
+K, T, S, N, R = 1024, 2048, 512, 256, 256
+FLOPS = 2 * (2 * K * S * N + S * R * N)
+
+F32 = mybir.dt.float32
+BF16 = mybir.dt.bfloat16
+I32 = mybir.dt.int32
+U32 = mybir.dt.uint32
+U16 = mybir.dt.uint16
+U8 = mybir.dt.uint8
+FP8X4 = mybir.dt.float8_e4m3fn_x4
+ALU = mybir.AluOpType
+ACT = mybir.ActivationFunctionType
+
+P = 128
+PACK = 4
+PASSES = K // (P * PACK)
+RUN = 8
+BLOCKS = S // (PACK * RUN)
+HALF = N // 2
+
+
+def weave(ap_out, ap_in):
+    return (ap_out.rearrange("p (c i) j -> p c j i", i=4), ap_in.rearrange("p j (c i) -> p c j i", i=4))
+
+
+def tile_picked_yrus_burg_p_kernel(tc, x_words, x_scales, cT, area, qm, cur, offs, right, out):
+    nc = tc.nc
+    with ExitStack() as ctx:
+        keep = ctx.enter_context(tc.tile_pool(name="keep", bufs=1))
+        psum = ctx.enter_context(tc.psum_pool(name="psum", bufs=1))
+
+        lists = [keep.tile([P, S // 16], U16, name=f"list{s}") for s in range(2)]
+        nc.sync.dma_start(lists[0][:], offs)
+        nc.sync.dma_start(lists[1][:], right)
+
+        scale_win = keep.tile([P, T], U8, name="scale_win", align_bytes=64)
+        nc.vector.memset(scale_win[:].bitcast(I32), 0)
+        for q in range(4):
+            nc.sync.dma_start(scale_win[32 * q : 32 * q + 4 * PASSES, :].bitcast(I32), x_scales[:, 4 * q : 4 * q + 4, :].bitcast(I32))
+
+        word_win = [keep.tile([P, T], U32, name=f"word_win{o}", align_bytes=64) for o in range(PASSES)]
+        c_rows = cT.rearrange("(o p j) m -> o p j m", o=PASSES, j=PACK)
+        c_raw0 = keep.tile([P, PACK, N], F32, name="c_raw0", align_bytes=64)
+        c_raw1 = [keep.tile([P, PACK, HALF], F32, name=f"c_raw1{h}", align_bytes=64) for h in range(2)]
+
+        def load_words(o):
+            nc.sync.dma_start(word_win[o][:].bitcast(I32), x_words[o].rearrange("p n t -> p (n t)").bitcast(I32))
+
+        load_words(0)
+        nc.sync.dma_start(c_raw0[:], c_rows[0])
+        nc.sync.dma_start(c_raw1[0][:], c_rows[1][:, :, 0:HALF])
+        load_words(1)
+        nc.sync.dma_start(c_raw1[1][:], c_rows[1][:, :, HALF:N])
+
+        q_raw = keep.tile([P, PACK, R], F32, name="q_raw", align_bytes=64)
+        q_rows = qm.rearrange("(g j i) r -> j g i r", j=PACK, i=RUN)
+        for j in range(PACK):
+            nc.sync.dma_start(q_raw[:, j, :], q_rows[j])
+        area_sb = keep.tile([P, PACK, 8], F32, name="area_sb", align_bytes=64)
+        area_rows = area.rearrange("(g j i) o -> j g i o", j=PACK, i=RUN)
+        with nc.allow_non_contiguous_dma(reason="one area a partition"):
+            for j in range(PACK):
+                nc.sync.dma_start(area_sb[:, j, 0:1], area_rows[j])
+        cur_sb = keep.tile([P, 2, N], F32, name="cur_sb", align_bytes=64)
+        nc.sync.dma_start(cur_sb[:], cur.rearrange("(a p) m -> p a m", p=P))
+
+        half_area = keep.tile([P, PACK], F32, name="half_area", align_bytes=64)
+        nc.gpsimd.tensor_scalar(half_area[:], area_sb[:, :, 0], 0.5, 0.0, ALU.mult, ALU.add)
+
+        x_planes = []
+        for s in range(2):
+            got = keep.tile([P, S], U8, name=f"scale_got{s}", align_bytes=64)
+            nc.vector.tensor_copy(got[:], scale_win[:].indirect(lists[s][:]))
+            plane = keep.tile([P, S], U8, name=f"x_plane{s}", align_bytes=64)
+            x_planes.append((got, plane))
+        for got, plane in x_planes:
+            nc.vector.tensor_copy(
+                plane[:].bitcast(I32).rearrange("p (j g h) -> p g j h", j=PACK, h=2),
+                got[:].bitcast(I32).rearrange("p (g j h) -> p g j h", j=PACK, h=2),
+            )
+
+        x_codes = [[keep.tile([P, S], U32, name=f"x_codes{s}{o}", align_bytes=64) for o in range(PASSES)] for s in range(2)]
+
+        def gather_words(s, o):
+            nc.vector.tensor_copy(
+                x_codes[s][o][:].rearrange("p (j g i) -> p g j i", j=PACK, i=RUN),
+                word_win[o][:].indirect(lists[s][:]),
+            )
+
+        c_bf = [keep.tile([P, N, PACK], BF16, name=f"c_bf{o}", align_bytes=64) for o in range(PASSES)]
+        c_codes = [keep.tile([P, N], U32, name=f"c_codes{o}", align_bytes=64) for o in range(PASSES)]
+        c_plane = [keep.tile([P, N], U8, name=f"c_plane{o}", align_bytes=64) for o in range(PASSES)]
+
+        def quantise(codes, plane, woven):
+            nc.vector.quantize_mx(out=codes.bitcast(FP8X4), scales=plane, in_=woven.rearrange("p n j -> p (n j)"))
+
+        banks = [[psum.tile([P, N], F32, name=f"state{s}{j}", tag=f"bank{s}{j}") for j in range(PACK)] for s in range(2)]
+
+        def products(s, o):
+            for j in range(PACK):
+                cols = slice(j * P, (j + 1) * P)
+                nc.tensor.matmul_mx(
+                    out=banks[s][j][:],
+                    lhsT=x_codes[s][o][:, cols].bitcast(FP8X4),
+                    lhsT_scale=x_planes[s][1][4 * o : P, cols],
+                    rhs=c_codes[o][:].bitcast(FP8X4),
+                    rhs_scale=c_plane[o][:],
+                    start=(o == 0),
+                    stop=(o == PASSES - 1),
+                )
+
+        nc.scalar.copy(*weave(c_bf[0][:], c_raw0[:]))
+        gather_words(0, 0)
+        gather_words(1, 0)
+        quantise(c_codes[0][:], c_plane[0][:], c_bf[0][:])
+        products(0, 0)
+        products(1, 0)
+        for h in range(2):
+            nc.scalar.copy(*weave(c_bf[1][:, h * HALF : (h + 1) * HALF, :], c_raw1[h][:]))
+        gather_words(0, 1)
+        quantise(c_codes[1][:], c_plane[1][:], c_bf[1][:])
+        products(0, 1)
+        gather_words(1, 1)
+        products(1, 1)
+
+        left = keep.tile([P, PACK, N], F32, name="left", align_bytes=64)
+        for j in range(PACK):
+            nc.scalar.copy(left[:, j, :], banks[0][j][:])
+
+        q_bf = keep.tile([P, R, PACK], BF16, name="q_bf", align_bytes=64)
+        q_codes = keep.tile([P, R], U32, name="q_codes", align_bytes=64)
+        q_plane = keep.tile([P, R], U8, name="q_plane", align_bytes=64)
+        nc.scalar.copy(*weave(q_bf[:], q_raw[:]))
+
+        peak = keep.tile([P, PACK, N], F32, name="peak", align_bytes=64)
+        drop = keep.tile([P, PACK, N], F32, name="drop", align_bytes=64)
+        peak_sq = keep.tile([P, PACK, N], F32, name="peak_sq", align_bytes=64)
+        drop_abs = keep.tile([P, PACK, N], F32, name="drop_abs", align_bytes=64)
+        term_a = keep.tile([P, PACK, N], F32, name="term_a", align_bytes=64)
+        term_b = keep.tile([P, PACK, N], F32, name="term_b", align_bytes=64)
+        for j in range(PACK):
+            nc.vector.tensor_tensor(drop[:, j, :], left[:, j, :], banks[1][j][:], ALU.subtract)
+            nc.vector.scalar_tensor_tensor(peak[:, j, :], banks[1][j][:], -1.0, left[:, j, :], ALU.mult, ALU.max)
+            nc.scalar.activation(drop_abs[:, j, :], drop[:, j, :], ACT.Abs, scale=0.5)
+            nc.scalar.activation(peak_sq[:, j, :], peak[:, j, :], ACT.Square)
+            nc.scalar.activation(term_a[:, j, :], peak_sq[:, j, :], ACT.Copy, scale=half_area[:, j : j + 1])
+        for j in range(PACK):
+            nc.vector.scalar_tensor_tensor(term_b[:, j, :], drop_abs[:, j, :], half_area[:, j : j + 1], drop[:, j, :], ALU.mult, ALU.mult)
+        quantise(q_codes[:], q_plane[:], q_bf[:])
+
+        fa_bf = [keep.tile([P, HALF, PACK], BF16, name=f"fa_bf{h}", align_bytes=64) for h in range(2)]
+        fa_codes = [keep.tile([P, HALF], U32, name=f"fa_codes{h}", align_bytes=64) for h in range(2)]
+        fa_plane = [keep.tile([P, HALF], U8, name=f"fa_plane{h}", align_bytes=64) for h in range(2)]
+        for h in range(2):
+            cols = slice(h * HALF, (h + 1) * HALF)
+            woven, a_view = weave(fa_bf[h][:], term_a[:, :, cols])
+            b_view = term_b[:, :, cols].rearrange("p j (c i) -> p c j i", i=4)
+            nc.vector.tensor_tensor(woven, a_view, b_view, ALU.add)
+        for h in range(2):
+            quantise(fa_codes[h][:], fa_plane[h][:], fa_bf[h][:])
+        out_rows = out.rearrange("(a p) m -> p a m", p=P)
+        for h in range(2):
+            cols = slice(h * HALF, (h + 1) * HALF)
+            acc = psum.tile([P, 2, HALF], F32, name=f"acc{h}", tag=f"bank0{h}")
+            for a in range(2):
+                rows = slice(a * P, (a + 1) * P)
+                nc.tensor.matmul_mx(
+                    out=acc[:, a, :],
+                    lhsT=q_codes[:, rows].bitcast(FP8X4),
+                    lhsT_scale=q_plane[:, rows],
+                    rhs=fa_codes[h][:].bitcast(FP8X4),
+                    rhs_scale=fa_plane[h][:],
+                    start=True,
+                    stop=True,
+                )
+            res = keep.tile([P, 2, HALF], F32, name=f"res{h}", align_bytes=64)
+            nc.vector.scalar_tensor_tensor(res[:], acc[:], -0.5, cur_sb[:, :, cols], ALU.mult, ALU.add)
+            queue = nc.sync if h == 0 else nc.scalar
+            queue.dma_start(out_rows[:, :, cols], res[:])

@@ -38,9 +38,7 @@ def tile_picked_yrus_burg_p_kernel(tc, x_words, x_scales, cT, area, qm, cur, off
         nc.sync.dma_start(lists[1][:], right)
 
         scale_win = keep.tile([P, T], U8, name="scale_win", align_bytes=64)
-        nc.vector.memset(scale_win[:].bitcast(I32), 0)
-        for q in range(4):
-            nc.sync.dma_start(scale_win[32 * q : 32 * q + 4 * PASSES, :].bitcast(I32), x_scales[:, 4 * q : 4 * q + 4, :].bitcast(I32))
+        nc.gpsimd.memset(scale_win[:].bitcast(I32), 0)
 
         word_win = [keep.tile([P, T], U32, name=f"word_win{o}", align_bytes=64) for o in range(PASSES)]
         c_rows = cT.rearrange("(o p j) m -> o p j m", o=PASSES, j=PACK)
@@ -50,16 +48,14 @@ def tile_picked_yrus_burg_p_kernel(tc, x_words, x_scales, cT, area, qm, cur, off
         def load_words(o):
             nc.sync.dma_start(word_win[o][:].bitcast(I32), x_words[o].rearrange("p n t -> p (n t)").bitcast(I32))
 
+        for q in range(4):
+            nc.sync.dma_start(scale_win[32 * q : 32 * q + 4 * PASSES, :].bitcast(I32), x_scales[:, 4 * q : 4 * q + 4, :].bitcast(I32))
         load_words(0)
         nc.sync.dma_start(c_raw0[:], c_rows[0])
         nc.sync.dma_start(c_raw1[0][:], c_rows[1][:, :, 0:HALF])
         load_words(1)
         nc.sync.dma_start(c_raw1[1][:], c_rows[1][:, :, HALF:N])
 
-        q_raw = keep.tile([P, PACK, R], F32, name="q_raw", align_bytes=64)
-        q_rows = qm.rearrange("(g j i) r -> j g i r", j=PACK, i=RUN)
-        for j in range(PACK):
-            nc.sync.dma_start(q_raw[:, j, :], q_rows[j])
         area_sb = keep.tile([P, PACK, 8], F32, name="area_sb", align_bytes=64)
         area_rows = area.rearrange("(g j i) o -> j g i o", j=PACK, i=RUN)
         with nc.allow_non_contiguous_dma(reason="one area a partition"):
@@ -68,30 +64,33 @@ def tile_picked_yrus_burg_p_kernel(tc, x_words, x_scales, cT, area, qm, cur, off
         cur_sb = keep.tile([P, 2, N], F32, name="cur_sb", align_bytes=64)
         nc.sync.dma_start(cur_sb[:], cur.rearrange("(a p) m -> p a m", p=P))
 
+        q_raw = keep.tile([P, PACK, R], F32, name="q_raw", align_bytes=64)
+        q_rows = qm.rearrange("(g j i) r -> j g i r", j=PACK, i=RUN)
+        for j in range(PACK):
+            nc.sync.dma_start(q_raw[:, j, :], q_rows[j])
         half_area = keep.tile([P, PACK], F32, name="half_area", align_bytes=64)
         nc.gpsimd.tensor_scalar(half_area[:], area_sb[:, :, 0], 0.5, 0.0, ALU.mult, ALU.add)
 
-        x_planes = []
-        for s in range(2):
+        x_planes = [keep.tile([P, S], U8, name=f"x_plane{s}", align_bytes=64) for s in range(2)]
+
+        def gather_scales(s):
             got = keep.tile([P, S], U8, name=f"scale_got{s}", align_bytes=64)
             nc.vector.tensor_copy(got[:], scale_win[:].indirect(lists[s][:]))
-            plane = keep.tile([P, S], U8, name=f"x_plane{s}", align_bytes=64)
-            x_planes.append((got, plane))
-        for got, plane in x_planes:
             nc.vector.tensor_copy(
-                plane[:].bitcast(I32).rearrange("p (j g h) -> p g j h", j=PACK, h=2),
+                x_planes[s][:].bitcast(I32).rearrange("p (j g h) -> p g j h", j=PACK, h=2),
                 got[:].bitcast(I32).rearrange("p (g j h) -> p g j h", j=PACK, h=2),
             )
 
-        x_codes = [[keep.tile([P, S], U32, name=f"x_codes{s}{o}", align_bytes=64) for o in range(PASSES)] for s in range(2)]
+        x_codes = {}
 
         def gather_words(s, o):
+            x_codes[s, o] = keep.tile([P, S], U32, name=f"x_codes{s}{o}", tag=f"c_bf{o}" if (s, o) == (1, 1) else f"x_codes{s}{o}", align_bytes=64)
             nc.vector.tensor_copy(
-                x_codes[s][o][:].rearrange("p (j g i) -> p g j i", j=PACK, i=RUN),
+                x_codes[s, o][:].rearrange("p (j g i) -> p g j i", j=PACK, i=RUN),
                 word_win[o][:].indirect(lists[s][:]),
             )
 
-        c_bf = [keep.tile([P, N, PACK], BF16, name=f"c_bf{o}", align_bytes=64) for o in range(PASSES)]
+        c_bf = [keep.tile([P, N, PACK], BF16, name=f"c_bf{o}", tag=f"c_bf{o}", align_bytes=64) for o in range(PASSES)]
         c_codes = [keep.tile([P, N], U32, name=f"c_codes{o}", align_bytes=64) for o in range(PASSES)]
         c_plane = [keep.tile([P, N], U8, name=f"c_plane{o}", align_bytes=64) for o in range(PASSES)]
 
@@ -105,8 +104,8 @@ def tile_picked_yrus_burg_p_kernel(tc, x_words, x_scales, cT, area, qm, cur, off
                 cols = slice(j * P, (j + 1) * P)
                 nc.tensor.matmul_mx(
                     out=banks[s][j][:],
-                    lhsT=x_codes[s][o][:, cols].bitcast(FP8X4),
-                    lhsT_scale=x_planes[s][1][4 * o : P, cols],
+                    lhsT=x_codes[s, o][:, cols].bitcast(FP8X4),
+                    lhsT_scale=x_planes[s][4 * o : P, cols],
                     rhs=c_codes[o][:].bitcast(FP8X4),
                     rhs_scale=c_plane[o][:],
                     start=(o == 0),
@@ -115,6 +114,8 @@ def tile_picked_yrus_burg_p_kernel(tc, x_words, x_scales, cT, area, qm, cur, off
 
         nc.scalar.copy(*weave(c_bf[0][:], c_raw0[:]))
         gather_words(0, 0)
+        gather_scales(0)
+        gather_scales(1)
         gather_words(1, 0)
         quantise(c_codes[0][:], c_plane[0][:], c_bf[0][:])
         products(0, 0)
@@ -127,14 +128,14 @@ def tile_picked_yrus_burg_p_kernel(tc, x_words, x_scales, cT, area, qm, cur, off
         gather_words(1, 1)
         products(1, 1)
 
-        left = keep.tile([P, PACK, N], F32, name="left", align_bytes=64)
-        for j in range(PACK):
-            nc.scalar.copy(left[:, j, :], banks[0][j][:])
-
         q_bf = keep.tile([P, R, PACK], BF16, name="q_bf", align_bytes=64)
         q_codes = keep.tile([P, R], U32, name="q_codes", align_bytes=64)
         q_plane = keep.tile([P, R], U8, name="q_plane", align_bytes=64)
-        nc.scalar.copy(*weave(q_bf[:], q_raw[:]))
+        nc.gpsimd.tensor_scalar(*weave(q_bf[:], q_raw[:]), 1.0, 0.0, ALU.mult, ALU.add)
+
+        left = keep.tile([P, PACK, N], F32, name="left", align_bytes=64)
+        for j in range(PACK):
+            nc.scalar.copy(left[:, j, :], banks[0][j][:])
 
         peak = keep.tile([P, PACK, N], F32, name="peak", align_bytes=64)
         drop = keep.tile([P, PACK, N], F32, name="drop", align_bytes=64)

@@ -56,6 +56,10 @@ def tile_picked_yrus_burg_p_kernel(tc, x_words, x_scales, cT, area, qm, cur, off
         load_words(1)
         nc.sync.dma_start(c_raw1[1][:], c_rows[1][:, :, HALF:N])
 
+        q_raw = keep.tile([P, PACK, R], F32, name="q_raw", align_bytes=64)
+        q_rows = qm.rearrange("(g j i) r -> j g i r", j=PACK, i=RUN)
+        for j in range(PACK):
+            nc.sync.dma_start(q_raw[:, j, :], q_rows[j])
         area_sb = keep.tile([P, PACK, 8], F32, name="area_sb", align_bytes=64)
         area_rows = area.rearrange("(g j i) o -> j g i o", j=PACK, i=RUN)
         with nc.allow_non_contiguous_dma(reason="one area a partition"):
@@ -64,10 +68,6 @@ def tile_picked_yrus_burg_p_kernel(tc, x_words, x_scales, cT, area, qm, cur, off
         cur_sb = keep.tile([P, 2, N], F32, name="cur_sb", align_bytes=64)
         nc.sync.dma_start(cur_sb[:], cur.rearrange("(a p) m -> p a m", p=P))
 
-        q_raw = keep.tile([P, PACK, R], F32, name="q_raw", align_bytes=64)
-        q_rows = qm.rearrange("(g j i) r -> j g i r", j=PACK, i=RUN)
-        for j in range(PACK):
-            nc.sync.dma_start(q_raw[:, j, :], q_rows[j])
         half_area = keep.tile([P, PACK], F32, name="half_area", align_bytes=64)
         nc.gpsimd.tensor_scalar(half_area[:], area_sb[:, :, 0], 0.5, 0.0, ALU.mult, ALU.add)
 
@@ -131,7 +131,6 @@ def tile_picked_yrus_burg_p_kernel(tc, x_words, x_scales, cT, area, qm, cur, off
         q_bf = keep.tile([P, R, PACK], BF16, name="q_bf", align_bytes=64)
         q_codes = keep.tile([P, R], U32, name="q_codes", align_bytes=64)
         q_plane = keep.tile([P, R], U8, name="q_plane", align_bytes=64)
-        nc.gpsimd.tensor_scalar(*weave(q_bf[:], q_raw[:]), 1.0, 0.0, ALU.mult, ALU.add)
 
         left = keep.tile([P, PACK, N], F32, name="left", align_bytes=64)
         for j in range(PACK):
@@ -141,26 +140,27 @@ def tile_picked_yrus_burg_p_kernel(tc, x_words, x_scales, cT, area, qm, cur, off
         drop = keep.tile([P, PACK, N], F32, name="drop", align_bytes=64)
         peak_sq = keep.tile([P, PACK, N], F32, name="peak_sq", align_bytes=64)
         drop_abs = keep.tile([P, PACK, N], F32, name="drop_abs", align_bytes=64)
-        term_a = keep.tile([P, PACK, N], F32, name="term_a", align_bytes=64)
         term_b = keep.tile([P, PACK, N], F32, name="term_b", align_bytes=64)
+        nc.scalar.copy(*weave(q_bf[:], q_raw[:]))
         for j in range(PACK):
             nc.vector.tensor_tensor(drop[:, j, :], left[:, j, :], banks[1][j][:], ALU.subtract)
             nc.vector.scalar_tensor_tensor(peak[:, j, :], banks[1][j][:], -1.0, left[:, j, :], ALU.mult, ALU.max)
             nc.scalar.activation(drop_abs[:, j, :], drop[:, j, :], ACT.Abs, scale=0.5)
             nc.scalar.activation(peak_sq[:, j, :], peak[:, j, :], ACT.Square)
-            nc.scalar.activation(term_a[:, j, :], peak_sq[:, j, :], ACT.Copy, scale=half_area[:, j : j + 1])
+        quantise(q_codes[:], q_plane[:], q_bf[:])
         for j in range(PACK):
             nc.vector.scalar_tensor_tensor(term_b[:, j, :], drop_abs[:, j, :], half_area[:, j : j + 1], drop[:, j, :], ALU.mult, ALU.mult)
-        quantise(q_codes[:], q_plane[:], q_bf[:])
 
+        fa_flat = [keep.tile([P, PACK, HALF], BF16, name=f"fa_flat{h}", align_bytes=64) for h in range(2)]
         fa_bf = [keep.tile([P, HALF, PACK], BF16, name=f"fa_bf{h}", align_bytes=64) for h in range(2)]
         fa_codes = [keep.tile([P, HALF], U32, name=f"fa_codes{h}", align_bytes=64) for h in range(2)]
         fa_plane = [keep.tile([P, HALF], U8, name=f"fa_plane{h}", align_bytes=64) for h in range(2)]
         for h in range(2):
             cols = slice(h * HALF, (h + 1) * HALF)
-            woven, a_view = weave(fa_bf[h][:], term_a[:, :, cols])
-            b_view = term_b[:, :, cols].rearrange("p j (c i) -> p c j i", i=4)
-            nc.vector.tensor_tensor(woven, a_view, b_view, ALU.add)
+            for j in range(PACK):
+                nc.vector.scalar_tensor_tensor(fa_flat[h][:, j, :], peak_sq[:, j, cols], half_area[:, j : j + 1], term_b[:, j, cols], ALU.mult, ALU.add)
+        nc.scalar.copy(*weave(fa_bf[0][:], fa_flat[0][:]))
+        nc.vector.tensor_copy(*weave(fa_bf[1][:], fa_flat[1][:]))
         for h in range(2):
             quantise(fa_codes[h][:], fa_plane[h][:], fa_bf[h][:])
         out_rows = out.rearrange("(a p) m -> p a m", p=P)

@@ -1,6 +1,8 @@
+import math
 from contextlib import ExitStack
 
 import concourse.mybir as mybir
+from concourse.masks import make_identity
 
 K, T, S, N, R = 1024, 2048, 512, 256, 256
 FLOPS = 2 * (2 * K * S * N + S * R * N)
@@ -18,13 +20,11 @@ ACT = mybir.ActivationFunctionType
 P = 128
 PACK = 4
 PASSES = K // (P * PACK)
-RUN = 8
-BLOCKS = S // (PACK * RUN)
-HALF = N // 2
+TILES = N // P
 
 
-def weave(ap_out, ap_in):
-    return (ap_out.rearrange("p (c i) j -> p c j i", i=4), ap_in.rearrange("p j (c i) -> p c j i", i=4))
+def weave(woven, rows):
+    return (woven.rearrange("p (c i) j -> p c j i", i=4), rows.rearrange("p j (c i) -> p c j i", i=4))
 
 
 def tile_picked_yrus_burg_p_kernel(tc, x_words, x_scales, cT, area, qm, cur, offs, right, out):
@@ -33,152 +33,145 @@ def tile_picked_yrus_burg_p_kernel(tc, x_words, x_scales, cT, area, qm, cur, off
         keep = ctx.enter_context(tc.tile_pool(name="keep", bufs=1))
         psum = ctx.enter_context(tc.psum_pool(name="psum", bufs=1))
 
+        def sbuf(name, shape, dtype, tag=None):
+            return keep.tile(shape, dtype, name=name, tag=tag or name, align_bytes=64)
+
         lists = [keep.tile([P, S // 16], U16, name=f"list{s}") for s in range(2)]
         nc.sync.dma_start(lists[0][:], offs)
         nc.sync.dma_start(lists[1][:], right)
 
-        scale_win = keep.tile([P, T], U8, name="scale_win", align_bytes=64)
+        scale_win = sbuf("scale_win", [P, T], U8)
         nc.gpsimd.memset(scale_win[:].bitcast(I32), 0)
+        for q in range(4):
+            nc.sync.dma_start(scale_win[32 * q : 32 * q + 4 * PASSES, :].bitcast(I32), x_scales[:, 4 * q : 4 * q + 4, :].bitcast(I32))
 
-        word_win = [keep.tile([P, T], U32, name=f"word_win{o}", align_bytes=64) for o in range(PASSES)]
+        word_win = [sbuf(f"word_win{o}", [P, T], U32) for o in range(PASSES)]
+        c_raw = [sbuf(f"c_raw{o}", [P, PACK, N], F32) for o in range(PASSES)]
         c_rows = cT.rearrange("(o p j) m -> o p j m", o=PASSES, j=PACK)
-        c_raw0 = keep.tile([P, PACK, N], F32, name="c_raw0", align_bytes=64)
-        c_raw1 = [keep.tile([P, PACK, HALF], F32, name=f"c_raw1{h}", align_bytes=64) for h in range(2)]
 
         def load_words(o):
             nc.sync.dma_start(word_win[o][:].bitcast(I32), x_words[o].rearrange("p n t -> p (n t)").bitcast(I32))
 
-        for q in range(4):
-            nc.sync.dma_start(scale_win[32 * q : 32 * q + 4 * PASSES, :].bitcast(I32), x_scales[:, 4 * q : 4 * q + 4, :].bitcast(I32))
         load_words(0)
-        nc.sync.dma_start(c_raw0[:], c_rows[0])
-        nc.sync.dma_start(c_raw1[0][:], c_rows[1][:, :, 0:HALF])
+        for o in range(PASSES):
+            nc.sync.dma_start(c_raw[o][:], c_rows[o])
         load_words(1)
-        nc.sync.dma_start(c_raw1[1][:], c_rows[1][:, :, HALF:N])
-
-        q_raw = keep.tile([P, PACK, R], F32, name="q_raw", align_bytes=64)
-        q_rows = qm.rearrange("(g j i) r -> j g i r", j=PACK, i=RUN)
-        for j in range(PACK):
-            nc.sync.dma_start(q_raw[:, j, :], q_rows[j])
-        area_sb = keep.tile([P, PACK, 8], F32, name="area_sb", align_bytes=64)
-        area_rows = area.rearrange("(g j i) o -> j g i o", j=PACK, i=RUN)
-        with nc.allow_non_contiguous_dma(reason="one area a partition"):
-            for j in range(PACK):
-                nc.sync.dma_start(area_sb[:, j, 0:1], area_rows[j])
-        cur_sb = keep.tile([P, 2, N], F32, name="cur_sb", align_bytes=64)
+        q_raw = sbuf("q_raw", [P, PACK, R], F32)
+        nc.sync.dma_start(q_raw[:], qm.rearrange("(p j) r -> p j r", j=PACK))
+        area_sb = sbuf("area_sb", [P, PACK], F32)
+        nc.sync.dma_start(area_sb[:], area.rearrange("(p j) o -> p (j o)", j=PACK))
+        cur_sb = sbuf("cur_sb", [P, R // P, N], F32)
         nc.sync.dma_start(cur_sb[:], cur.rearrange("(a p) m -> p a m", p=P))
 
-        half_area = keep.tile([P, PACK], F32, name="half_area", align_bytes=64)
-        nc.gpsimd.tensor_scalar(half_area[:], area_sb[:, :, 0], 0.5, 0.0, ALU.mult, ALU.add)
+        ident = sbuf("ident", [P, P], F32)
+        make_identity(nc, ident[:])
 
-        x_planes = [keep.tile([P, S], U8, name=f"x_plane{s}", align_bytes=64) for s in range(2)]
-
-        def gather_scales(s):
-            got = keep.tile([P, S], U8, name=f"scale_got{s}", align_bytes=64)
-            nc.vector.tensor_copy(got[:], scale_win[:].indirect(lists[s][:]))
-            nc.vector.tensor_copy(
-                x_planes[s][:].bitcast(I32).rearrange("p (j g h) -> p g j h", j=PACK, h=2),
-                got[:].bitcast(I32).rearrange("p (g j h) -> p g j h", j=PACK, h=2),
-            )
-
-        x_codes = {}
-
-        def gather_words(s, o):
-            x_codes[s, o] = keep.tile([P, S], U32, name=f"x_codes{s}{o}", tag=f"c_bf{o}" if (s, o) == (1, 1) else f"x_codes{s}{o}", align_bytes=64)
-            nc.vector.tensor_copy(
-                x_codes[s, o][:].rearrange("p (j g i) -> p g j i", j=PACK, i=RUN),
-                word_win[o][:].indirect(lists[s][:]),
-            )
-
-        c_bf = [keep.tile([P, N, PACK], BF16, name=f"c_bf{o}", tag=f"c_bf{o}", align_bytes=64) for o in range(PASSES)]
-        c_codes = [keep.tile([P, N], U32, name=f"c_codes{o}", align_bytes=64) for o in range(PASSES)]
-        c_plane = [keep.tile([P, N], U8, name=f"c_plane{o}", align_bytes=64) for o in range(PASSES)]
+        x_plane = [sbuf(f"x_plane{s}", [P, S], U8) for s in range(2)]
+        x_codes = [[sbuf(f"x_codes{s}{o}", [P, S], U32) for o in range(PASSES)] for s in range(2)]
+        c_bf = [sbuf(f"c_bf{o}", [P, N, PACK], BF16) for o in range(PASSES)]
+        c_codes = [sbuf(f"c_codes{o}", [P, N], U32) for o in range(PASSES)]
+        c_plane = [sbuf(f"c_plane{o}", [P, N], U8) for o in range(PASSES)]
+        state = [[psum.tile([P, S], F32, name=f"state{s}{b}") for b in range(TILES)] for s in range(2)]
 
         def quantise(codes, plane, woven):
             nc.vector.quantize_mx(out=codes.bitcast(FP8X4), scales=plane, in_=woven.rearrange("p n j -> p (n j)"))
 
-        banks = [[psum.tile([P, N], F32, name=f"state{s}{j}", tag=f"bank{s}{j}") for j in range(PACK)] for s in range(2)]
+        def gather_words(s, o):
+            nc.vector.tensor_copy(x_codes[s][o][:], word_win[o][:].indirect(lists[s][:]))
 
         def products(s, o):
-            for j in range(PACK):
-                cols = slice(j * P, (j + 1) * P)
+            for b in range(TILES):
+                cols = slice(b * P, (b + 1) * P)
                 nc.tensor.matmul_mx(
-                    out=banks[s][j][:],
-                    lhsT=x_codes[s, o][:, cols].bitcast(FP8X4),
-                    lhsT_scale=x_planes[s][4 * o : P, cols],
-                    rhs=c_codes[o][:].bitcast(FP8X4),
-                    rhs_scale=c_plane[o][:],
+                    out=state[s][b][:],
+                    lhsT=c_codes[o][:, cols].bitcast(FP8X4),
+                    lhsT_scale=c_plane[o][:, cols],
+                    rhs=x_codes[s][o][:].bitcast(FP8X4),
+                    rhs_scale=x_plane[s][4 * o : P, :],
                     start=(o == 0),
                     stop=(o == PASSES - 1),
                 )
 
-        nc.scalar.copy(*weave(c_bf[0][:], c_raw0[:]))
-        gather_words(0, 0)
-        gather_scales(0)
-        gather_scales(1)
-        gather_words(1, 0)
-        quantise(c_codes[0][:], c_plane[0][:], c_bf[0][:])
-        products(0, 0)
-        products(1, 0)
-        for h in range(2):
-            nc.scalar.copy(*weave(c_bf[1][:, h * HALF : (h + 1) * HALF, :], c_raw1[h][:]))
-        gather_words(0, 1)
-        quantise(c_codes[1][:], c_plane[1][:], c_bf[1][:])
-        products(0, 1)
-        gather_words(1, 1)
-        products(1, 1)
+        for s in range(2):
+            nc.vector.tensor_copy(x_plane[s][:], scale_win[:].indirect(lists[s][:]))
+        for s in range(2):
+            gather_words(s, 0)
+        for o in range(PASSES):
+            nc.scalar.copy(*weave(c_bf[o][:], c_raw[o][:]))
+            quantise(c_codes[o][:], c_plane[o][:], c_bf[o][:])
+        for s in range(2):
+            products(s, 0)
+        for s in range(2):
+            gather_words(s, 1)
+            products(s, 1)
 
-        q_bf = keep.tile([P, R, PACK], BF16, name="q_bf", align_bytes=64)
-        q_codes = keep.tile([P, R], U32, name="q_codes", align_bytes=64)
-        q_plane = keep.tile([P, R], U8, name="q_plane", align_bytes=64)
-
-        left = keep.tile([P, PACK, N], F32, name="left", align_bytes=64)
-        for j in range(PACK):
-            nc.scalar.copy(left[:, j, :], banks[0][j][:])
-
-        peak = keep.tile([P, PACK, N], F32, name="peak", align_bytes=64)
-        drop = keep.tile([P, PACK, N], F32, name="drop", align_bytes=64)
-        peak_sq = keep.tile([P, PACK, N], F32, name="peak_sq", align_bytes=64)
-        drop_abs = keep.tile([P, PACK, N], F32, name="drop_abs", align_bytes=64)
-        term_b = keep.tile([P, PACK, N], F32, name="term_b", align_bytes=64)
+        q_bf = sbuf("q_bf", [P, R, PACK], BF16)
+        q_codes = sbuf("q_codes", [P, R], U32)
+        q_plane = sbuf("q_plane", [P, R], U8)
         nc.scalar.copy(*weave(q_bf[:], q_raw[:]))
-        for j in range(PACK):
-            nc.vector.tensor_tensor(drop[:, j, :], left[:, j, :], banks[1][j][:], ALU.subtract)
-            nc.vector.scalar_tensor_tensor(peak[:, j, :], banks[1][j][:], -1.0, left[:, j, :], ALU.mult, ALU.max)
-            nc.scalar.activation(drop_abs[:, j, :], drop[:, j, :], ACT.Abs, scale=0.5)
-            nc.scalar.activation(peak_sq[:, j, :], peak[:, j, :], ACT.Square)
         quantise(q_codes[:], q_plane[:], q_bf[:])
-        for j in range(PACK):
-            nc.vector.scalar_tensor_tensor(term_b[:, j, :], drop_abs[:, j, :], half_area[:, j : j + 1], drop[:, j, :], ALU.mult, ALU.mult)
 
-        fa_flat = [keep.tile([P, PACK, HALF], BF16, name=f"fa_flat{h}", align_bytes=64) for h in range(2)]
-        fa_bf = [keep.tile([P, HALF, PACK], BF16, name=f"fa_bf{h}", align_bytes=64) for h in range(2)]
-        fa_codes = [keep.tile([P, HALF], U32, name=f"fa_codes{h}", align_bytes=64) for h in range(2)]
-        fa_plane = [keep.tile([P, HALF], U8, name=f"fa_plane{h}", align_bytes=64) for h in range(2)]
-        for h in range(2):
-            cols = slice(h * HALF, (h + 1) * HALF)
+        def by_slot(bank):
+            return bank[:].rearrange("p (q j) -> p j q", j=PACK)
+
+        shape = [P, PACK, P]
+        left = [sbuf(f"left{b}", shape, F32) for b in range(TILES)]
+        drop = [sbuf(f"drop{b}", shape, F32) for b in range(TILES)]
+        drop_abs = [sbuf(f"drop_abs{b}", shape, F32) for b in range(TILES)]
+        term_a = [sbuf(f"term_a{b}", shape, F32) for b in range(TILES)]
+        term_b = [sbuf(f"term_b{b}", shape, F32) for b in range(TILES)]
+        for b in range(TILES):
+            nc.scalar.copy(left[b][:], by_slot(state[0][b]))
+        flux = [psum.tile(shape, F32, name=f"flux{b}") for b in range(TILES)]
+        fa_bf = [sbuf(f"fa_bf{b}", [P, P, PACK], BF16) for b in range(TILES)]
+        fa_codes = [sbuf(f"fa_codes{b}", [P, P], U32) for b in range(TILES)]
+        fa_plane = [sbuf(f"fa_plane{b}", [P, P], U8) for b in range(TILES)]
+        area_wide = area_sb[:].unsqueeze(1).to_broadcast([P, P, PACK])
+
+        def make_drop(b):
+            nc.vector.tensor_tensor(drop[b][:], left[b][:], by_slot(state[1][b]), ALU.subtract)
+            nc.scalar.activation(drop_abs[b][:], drop[b][:], ACT.Abs, scale=0.25)
+
+        def make_peak(b):
+            peak = sbuf(f"peak{b}", shape, F32, tag=f"drop_abs{b - 1}" if b else None)
+            nc.vector.scalar_tensor_tensor(peak[:], by_slot(state[1][b]), -1.0, left[b][:], ALU.mult, ALU.max)
+            nc.scalar.activation(term_a[b][:], peak[:], ACT.Square, scale=math.sqrt(0.5))
+
+        def make_signed(b):
+            nc.vector.tensor_tensor(term_b[b][:], drop_abs[b][:], drop[b][:], ALU.mult)
+
+        def turn(b):
             for j in range(PACK):
-                nc.vector.scalar_tensor_tensor(fa_flat[h][:, j, :], peak_sq[:, j, cols], half_area[:, j : j + 1], term_b[:, j, cols], ALU.mult, ALU.add)
-        nc.scalar.copy(*weave(fa_bf[0][:], fa_flat[0][:]))
-        nc.vector.tensor_copy(*weave(fa_bf[1][:], fa_flat[1][:]))
-        for h in range(2):
-            quantise(fa_codes[h][:], fa_plane[h][:], fa_bf[h][:])
+                nc.tensor.matmul(flux[b][:, j, :], term_a[b][:, j, :], ident[:], start=True, stop=False, is_transpose=True)
+                nc.tensor.matmul(flux[b][:, j, :], term_b[b][:, j, :], ident[:], start=False, stop=True, is_transpose=True)
+
+        make_drop(0)
+        make_peak(0)
+        make_signed(0)
+        turn(0)
+        make_drop(1)
+        make_peak(1)
+        make_signed(1)
+        turn(1)
+        for b in range(TILES):
+            nc.vector.tensor_tensor(fa_bf[b][:], flux[b][:].rearrange("p j m -> p m j"), area_wide, ALU.mult)
+            quantise(fa_codes[b][:], fa_plane[b][:], fa_bf[b][:])
         out_rows = out.rearrange("(a p) m -> p a m", p=P)
-        for h in range(2):
-            cols = slice(h * HALF, (h + 1) * HALF)
-            acc = psum.tile([P, 2, HALF], F32, name=f"acc{h}", tag=f"bank0{h}")
-            for a in range(2):
+        for b in range(TILES):
+            cols = slice(b * P, (b + 1) * P)
+            acc = psum.tile([P, R // P, P], F32, name=f"acc{b}")
+            for a in range(R // P):
                 rows = slice(a * P, (a + 1) * P)
                 nc.tensor.matmul_mx(
                     out=acc[:, a, :],
                     lhsT=q_codes[:, rows].bitcast(FP8X4),
                     lhsT_scale=q_plane[:, rows],
-                    rhs=fa_codes[h][:].bitcast(FP8X4),
-                    rhs_scale=fa_plane[h][:],
+                    rhs=fa_codes[b][:].bitcast(FP8X4),
+                    rhs_scale=fa_plane[b][:],
                     start=True,
                     stop=True,
                 )
-            res = keep.tile([P, 2, HALF], F32, name=f"res{h}", align_bytes=64)
+            res = sbuf(f"res{b}", [P, R // P, P], F32)
             nc.vector.scalar_tensor_tensor(res[:], acc[:], -0.5, cur_sb[:, :, cols], ALU.mult, ALU.add)
-            queue = nc.sync if h == 0 else nc.scalar
+            queue = nc.sync if b == 0 else nc.scalar
             queue.dma_start(out_rows[:, :, cols], res[:])

@@ -37,13 +37,9 @@ def tile_picked_yrus_burg_p_kernel(tc, x_words, x_scales, cT, area, qm, cur, off
             return keep.tile(shape, dtype, name=name, tag=tag or name, align_bytes=64)
 
         lists = [keep.tile([P, S // 16], U16, name=f"list{s}") for s in range(2)]
-        nc.sync.dma_start(lists[0][:], offs)
-        nc.sync.dma_start(lists[1][:], right)
 
         scale_win = sbuf("scale_win", [P, T], U8)
         nc.gpsimd.memset(scale_win[:].bitcast(I32), 0)
-        for q in range(4):
-            nc.sync.dma_start(scale_win[32 * q : 32 * q + 4 * PASSES, :].bitcast(I32), x_scales[:, 4 * q : 4 * q + 4, :].bitcast(I32))
 
         word_win = [sbuf(f"word_win{o}", [P, T], U32) for o in range(PASSES)]
         c_raw = [sbuf(f"c_raw{o}", [P, PACK, N], F32) for o in range(PASSES)]
@@ -53,11 +49,15 @@ def tile_picked_yrus_burg_p_kernel(tc, x_words, x_scales, cT, area, qm, cur, off
             nc.sync.dma_start(word_win[o][:].bitcast(I32), x_words[o].rearrange("p n t -> p (n t)").bitcast(I32))
 
         load_words(0)
+        nc.sync.dma_start(lists[0][:], offs)
+        nc.sync.dma_start(lists[1][:], right)
+        for q in range(4):
+            nc.gpsimd.dma_start(scale_win[32 * q : 32 * q + 4 * PASSES, :].bitcast(I32), x_scales[:, 4 * q : 4 * q + 4, :].bitcast(I32))
         for o in range(PASSES):
             nc.sync.dma_start(c_raw[o][:], c_rows[o])
-        load_words(1)
         q_raw = sbuf("q_raw", [P, PACK, R], F32)
         nc.sync.dma_start(q_raw[:], qm.rearrange("(p j) r -> p j r", j=PACK))
+        load_words(1)
         area_sb = sbuf("area_sb", [P, PACK], F32)
         nc.sync.dma_start(area_sb[:], area.rearrange("(p j) o -> p (j o)", j=PACK))
         cur_sb = sbuf("cur_sb", [P, R // P, N], F32)
@@ -66,53 +66,66 @@ def tile_picked_yrus_burg_p_kernel(tc, x_words, x_scales, cT, area, qm, cur, off
         ident = sbuf("ident", [P, P], F32)
         make_identity(nc, ident[:])
 
-        x_plane = [sbuf(f"x_plane{s}", [P, S], U8) for s in range(2)]
-        x_codes = [[sbuf(f"x_codes{s}{o}", [P, S], U32) for o in range(PASSES)] for s in range(2)]
+        x_codes = [[sbuf(f"x_codes{s}{o}", [P, S], U32, tag=f"x_codes{s}") for o in range(PASSES)] for s in range(2)]
         c_bf = [sbuf(f"c_bf{o}", [P, N, PACK], BF16) for o in range(PASSES)]
+        x_plane = [sbuf(f"x_plane{s}", [P, S], U8, tag="c_bf0" if s else None) for s in range(2)]
         c_codes = [sbuf(f"c_codes{o}", [P, N], U32) for o in range(PASSES)]
         c_plane = [sbuf(f"c_plane{o}", [P, N], U8) for o in range(PASSES)]
-        state = [[psum.tile([P, S], F32, name=f"state{s}{b}") for b in range(TILES)] for s in range(2)]
+        HALF = S // 2
+        whole = [slice(0, S)]
+        halves = [slice(0, HALF), slice(HALF, S)]
+        spans = {(0, 0): whole, (0, 1): whole, (1, 0): halves, (1, 1): whole}
+        state = {
+            (s, b, span.start): psum.tile([P, span.stop - span.start], F32, name=f"state{s}{b}{span.start}")
+            for (s, b), cut in spans.items()
+            for span in cut
+        }
 
         def quantise(codes, plane, woven):
             nc.vector.quantize_mx(out=codes.bitcast(FP8X4), scales=plane, in_=woven.rearrange("p n j -> p (n j)"))
 
-        def gather_words(s, o):
-            nc.vector.tensor_copy(x_codes[s][o][:], word_win[o][:].indirect(lists[s][:]))
+        def gather_words(s, o, span=whole[0]):
+            nc.vector.tensor_copy(x_codes[s][o][:, span], word_win[o][:].indirect(lists[s][:, span.start // 16 : span.stop // 16]))
+
+        def product(s, o, b, span):
+            cols = slice(b * P, (b + 1) * P)
+            nc.tensor.matmul_mx(
+                out=state[s, b, span.start][:],
+                lhsT=c_codes[o][:, cols].bitcast(FP8X4),
+                lhsT_scale=c_plane[o][:, cols],
+                rhs=x_codes[s][o][:, span].bitcast(FP8X4),
+                rhs_scale=x_plane[s][4 * o : P, span],
+                start=(o == 0),
+                stop=(o == PASSES - 1),
+            )
 
         def products(s, o):
             for b in range(TILES):
-                cols = slice(b * P, (b + 1) * P)
-                nc.tensor.matmul_mx(
-                    out=state[s][b][:],
-                    lhsT=c_codes[o][:, cols].bitcast(FP8X4),
-                    lhsT_scale=c_plane[o][:, cols],
-                    rhs=x_codes[s][o][:].bitcast(FP8X4),
-                    rhs_scale=x_plane[s][4 * o : P, :],
-                    start=(o == 0),
-                    stop=(o == PASSES - 1),
-                )
+                for span in spans[s, b]:
+                    product(s, o, b, span)
 
-        for s in range(2):
-            nc.vector.tensor_copy(x_plane[s][:], scale_win[:].indirect(lists[s][:]))
         for s in range(2):
             gather_words(s, 0)
         for o in range(PASSES):
             nc.scalar.copy(*weave(c_bf[o][:], c_raw[o][:]))
-            quantise(c_codes[o][:], c_plane[o][:], c_bf[o][:])
-        for s in range(2):
-            products(s, 0)
-        for s in range(2):
-            gather_words(s, 1)
-            products(s, 1)
-
         q_bf = sbuf("q_bf", [P, R, PACK], BF16)
-        q_codes = sbuf("q_codes", [P, R], U32)
-        q_plane = sbuf("q_plane", [P, R], U8)
         nc.scalar.copy(*weave(q_bf[:], q_raw[:]))
-        quantise(q_codes[:], q_plane[:], q_bf[:])
+        for s in range(2):
+            nc.vector.tensor_copy(x_plane[s][:], scale_win[:].indirect(lists[s][:]))
+            quantise(c_codes[s][:], c_plane[s][:], c_bf[s][:])
+            products(s, 0)
+        gather_words(0, 1)
+        products(0, 1)
+        for span in halves:
+            gather_words(1, 1, span)
+            product(1, 1, 0, span)
+        product(1, 1, 1, whole[0])
 
         def by_slot(bank):
             return bank[:].rearrange("p (q j) -> p j q", j=PACK)
+
+        def part(tile, span):
+            return tile[:, :, span.start // PACK : span.stop // PACK]
 
         shape = [P, PACK, P]
         left = [sbuf(f"left{b}", shape, F32) for b in range(TILES)]
@@ -121,45 +134,43 @@ def tile_picked_yrus_burg_p_kernel(tc, x_words, x_scales, cT, area, qm, cur, off
         term_a = [sbuf(f"term_a{b}", shape, F32) for b in range(TILES)]
         term_b = [sbuf(f"term_b{b}", shape, F32) for b in range(TILES)]
         for b in range(TILES):
-            nc.scalar.copy(left[b][:], by_slot(state[0][b]))
+            nc.scalar.copy(left[b][:], by_slot(state[0, b, 0]))
         flux = [psum.tile(shape, F32, name=f"flux{b}") for b in range(TILES)]
         fa_bf = [sbuf(f"fa_bf{b}", [P, P, PACK], BF16) for b in range(TILES)]
         fa_codes = [sbuf(f"fa_codes{b}", [P, P], U32) for b in range(TILES)]
         fa_plane = [sbuf(f"fa_plane{b}", [P, P], U8) for b in range(TILES)]
         area_wide = area_sb[:].unsqueeze(1).to_broadcast([P, P, PACK])
 
-        def make_drop(b):
-            nc.vector.tensor_tensor(drop[b][:], left[b][:], by_slot(state[1][b]), ALU.subtract)
+        peak = [sbuf(f"peak{b}", shape, F32) for b in range(TILES)]
+
+        def combine(b):
+            for span in spans[1, b]:
+                other = by_slot(state[1, b, span.start])
+                nc.vector.tensor_tensor(part(drop[b], span), part(left[b], span), other, ALU.subtract)
+                nc.vector.scalar_tensor_tensor(part(peak[b], span), other, -1.0, part(left[b], span), ALU.mult, ALU.max)
             nc.scalar.activation(drop_abs[b][:], drop[b][:], ACT.Abs, scale=0.25)
-
-        def make_peak(b):
-            peak = sbuf(f"peak{b}", shape, F32, tag=f"drop_abs{b - 1}" if b else None)
-            nc.vector.scalar_tensor_tensor(peak[:], by_slot(state[1][b]), -1.0, left[b][:], ALU.mult, ALU.max)
-            nc.scalar.activation(term_a[b][:], peak[:], ACT.Square, scale=math.sqrt(0.5))
-
-        def make_signed(b):
-            nc.vector.tensor_tensor(term_b[b][:], drop_abs[b][:], drop[b][:], ALU.mult)
+            nc.scalar.activation(term_a[b][:], peak[b][:], ACT.Square, scale=math.sqrt(0.5))
 
         def turn(b):
-            for j in range(PACK):
-                nc.tensor.matmul(flux[b][:, j, :], term_a[b][:, j, :], ident[:], start=True, stop=False, is_transpose=True)
-                nc.tensor.matmul(flux[b][:, j, :], term_b[b][:, j, :], ident[:], start=False, stop=True, is_transpose=True)
+            for n, term in enumerate((term_a[b], term_b[b])):
+                for j in range(PACK):
+                    nc.tensor.matmul(flux[b][:, j, :], term[:, j, :], ident[:], start=(n, j) == (0, 0), stop=(n, j) == (1, PACK - 1), is_transpose=True)
 
-        make_drop(0)
-        make_peak(0)
-        make_signed(0)
-        turn(0)
-        make_drop(1)
-        make_peak(1)
-        make_signed(1)
-        turn(1)
+        for b in range(TILES):
+            combine(b)
+        q_codes = sbuf("q_codes", [P, R], U32, tag="left1")
+        q_plane = sbuf("q_plane", [P, R], U8)
+        quantise(q_codes[:], q_plane[:], q_bf[:])
+        for b in range(TILES):
+            nc.vector.tensor_tensor(term_b[b][:], drop_abs[b][:], drop[b][:], ALU.mult)
+            turn(b)
         for b in range(TILES):
             nc.vector.tensor_tensor(fa_bf[b][:], flux[b][:].rearrange("p j m -> p m j"), area_wide, ALU.mult)
             quantise(fa_codes[b][:], fa_plane[b][:], fa_bf[b][:])
         out_rows = out.rearrange("(a p) m -> p a m", p=P)
         for b in range(TILES):
             cols = slice(b * P, (b + 1) * P)
-            acc = psum.tile([P, R // P, P], F32, name=f"acc{b}")
+            acc = psum.tile([P, R // P, P], F32, name=f"acc{b}", tag=f"state0{b}0")
             for a in range(R // P):
                 rows = slice(a * P, (a + 1) * P)
                 nc.tensor.matmul_mx(

@@ -48,16 +48,16 @@ def tile_picked_yrus_burg_p_kernel(tc, x_words, x_scales, cT, area, qm, cur, off
         def load_words(o):
             nc.sync.dma_start(word_win[o][:].bitcast(I32), x_words[o].rearrange("p n t -> p (n t)").bitcast(I32))
 
-        load_words(0)
         nc.sync.dma_start(lists[0][:], offs)
         nc.sync.dma_start(lists[1][:], right)
         for q in range(4):
-            nc.gpsimd.dma_start(scale_win[32 * q : 32 * q + 4 * PASSES, :].bitcast(I32), x_scales[:, 4 * q : 4 * q + 4, :].bitcast(I32))
+            nc.sync.dma_start(scale_win[32 * q : 32 * q + 4 * PASSES, :].bitcast(I32), x_scales[:, 4 * q : 4 * q + 4, :].bitcast(I32))
+        load_words(0)
         for o in range(PASSES):
             nc.sync.dma_start(c_raw[o][:], c_rows[o])
+        load_words(1)
         q_raw = sbuf("q_raw", [P, PACK, R], F32)
         nc.sync.dma_start(q_raw[:], qm.rearrange("(p j) r -> p j r", j=PACK))
-        load_words(1)
         area_sb = sbuf("area_sb", [P, PACK], F32)
         nc.sync.dma_start(area_sb[:], area.rearrange("(p j) o -> p (j o)", j=PACK))
         cur_sb = sbuf("cur_sb", [P, R // P, N], F32)
@@ -68,7 +68,7 @@ def tile_picked_yrus_burg_p_kernel(tc, x_words, x_scales, cT, area, qm, cur, off
 
         x_codes = [[sbuf(f"x_codes{s}{o}", [P, S], U32, tag=f"x_codes{s}") for o in range(PASSES)] for s in range(2)]
         c_bf = [sbuf(f"c_bf{o}", [P, N, PACK], BF16) for o in range(PASSES)]
-        x_plane = [sbuf(f"x_plane{s}", [P, S], U8, tag="c_bf0" if s else None) for s in range(2)]
+        x_plane = [sbuf(f"x_plane{s}", [P, S], U8) for s in range(2)]
         c_codes = [sbuf(f"c_codes{o}", [P, N], U32) for o in range(PASSES)]
         c_plane = [sbuf(f"c_plane{o}", [P, N], U8) for o in range(PASSES)]
         HALF = S // 2
@@ -105,14 +105,13 @@ def tile_picked_yrus_burg_p_kernel(tc, x_words, x_scales, cT, area, qm, cur, off
                     product(s, o, b, span)
 
         for s in range(2):
+            nc.vector.tensor_copy(x_plane[s][:], scale_win[:].indirect(lists[s][:]))
+        for s in range(2):
             gather_words(s, 0)
         for o in range(PASSES):
             nc.scalar.copy(*weave(c_bf[o][:], c_raw[o][:]))
-        q_bf = sbuf("q_bf", [P, R, PACK], BF16)
-        nc.scalar.copy(*weave(q_bf[:], q_raw[:]))
+            quantise(c_codes[o][:], c_plane[o][:], c_bf[o][:])
         for s in range(2):
-            nc.vector.tensor_copy(x_plane[s][:], scale_win[:].indirect(lists[s][:]))
-            quantise(c_codes[s][:], c_plane[s][:], c_bf[s][:])
             products(s, 0)
         gather_words(0, 1)
         products(0, 1)
@@ -158,6 +157,8 @@ def tile_picked_yrus_burg_p_kernel(tc, x_words, x_scales, cT, area, qm, cur, off
 
         for b in range(TILES):
             combine(b)
+        q_bf = sbuf("q_bf", [P, R, PACK], BF16, tag="word_win1")
+        nc.gpsimd.tensor_scalar(q_bf[:], q_raw[:].rearrange("p j r -> p r j"), 1.0, 0.0, ALU.mult, ALU.add)
         q_codes = sbuf("q_codes", [P, R], U32, tag="left1")
         q_plane = sbuf("q_plane", [P, R], U8)
         quantise(q_codes[:], q_plane[:], q_bf[:])

@@ -133,38 +133,39 @@ def tile_picked_yrus_burg_p_kernel(tc, x_words, x_scales, cT, area, qm, cur, off
         term_a = [sbuf(f"term_a{b}", shape, F32) for b in range(TILES)]
         term_b = [sbuf(f"term_b{b}", shape, F32) for b in range(TILES)]
         for b in range(TILES):
-            nc.scalar.copy(left[b][:], by_slot(state[0, b, 0]))
+            for span in spans[1, b]:
+                nc.scalar.copy(part(left[b], span), part(by_slot(state[0, b, 0]), span))
         flux = [psum.tile(shape, F32, name=f"flux{b}") for b in range(TILES)]
         fa_bf = [sbuf(f"fa_bf{b}", [P, P, PACK], BF16) for b in range(TILES)]
         fa_codes = [sbuf(f"fa_codes{b}", [P, P], U32) for b in range(TILES)]
         fa_plane = [sbuf(f"fa_plane{b}", [P, P], U8) for b in range(TILES)]
         area_wide = area_sb[:].unsqueeze(1).to_broadcast([P, P, PACK])
 
-        peak = [sbuf(f"peak{b}", shape, F32) for b in range(TILES)]
+        peak = [sbuf(f"peak{b}", shape, F32, tag=f"peak{b}") for b in range(TILES)]
 
         def combine(b):
             for span in spans[1, b]:
                 other = by_slot(state[1, b, span.start])
                 nc.vector.tensor_tensor(part(drop[b], span), part(left[b], span), other, ALU.subtract)
                 nc.vector.scalar_tensor_tensor(part(peak[b], span), other, -1.0, part(left[b], span), ALU.mult, ALU.max)
-            nc.scalar.activation(drop_abs[b][:], drop[b][:], ACT.Abs, scale=0.25)
-            nc.scalar.activation(term_a[b][:], peak[b][:], ACT.Square, scale=math.sqrt(0.5))
+                nc.scalar.activation(part(drop_abs[b], span), part(drop[b], span), ACT.Abs, scale=0.25)
+                nc.scalar.activation(part(term_a[b], span), part(peak[b], span), ACT.Square, scale=math.sqrt(0.5))
+                engine = nc.vector if b else nc.gpsimd
+                engine.tensor_tensor(part(term_b[b], span), part(drop_abs[b], span), part(drop[b], span), ALU.mult)
 
         def turn(b):
             for n, term in enumerate((term_a[b], term_b[b])):
                 for j in range(PACK):
                     nc.tensor.matmul(flux[b][:, j, :], term[:, j, :], ident[:], start=(n, j) == (0, 0), stop=(n, j) == (1, PACK - 1), is_transpose=True)
 
-        for b in range(TILES):
-            combine(b)
         q_bf = sbuf("q_bf", [P, R, PACK], BF16, tag="word_win1")
         nc.gpsimd.tensor_scalar(q_bf[:], q_raw[:].rearrange("p j r -> p r j"), 1.0, 0.0, ALU.mult, ALU.add)
+        for b in range(TILES):
+            combine(b)
+            turn(b)
         q_codes = sbuf("q_codes", [P, R], U32, tag="left1")
         q_plane = sbuf("q_plane", [P, R], U8)
         quantise(q_codes[:], q_plane[:], q_bf[:])
-        for b in range(TILES):
-            nc.vector.tensor_tensor(term_b[b][:], drop_abs[b][:], drop[b][:], ALU.mult)
-            turn(b)
         for b in range(TILES):
             nc.vector.tensor_tensor(fa_bf[b][:], flux[b][:].rearrange("p j m -> p m j"), area_wide, ALU.mult)
             quantise(fa_codes[b][:], fa_plane[b][:], fa_bf[b][:])

@@ -150,8 +150,6 @@ def tile_picked_yrus_burg_p_kernel(tc, x_words, x_scales, cT, area, qm, cur, off
                 nc.vector.scalar_tensor_tensor(part(peak[b], span), other, -1.0, part(left[b], span), ALU.mult, ALU.max)
                 nc.scalar.activation(part(drop_abs[b], span), part(drop[b], span), ACT.Abs, scale=0.25)
                 nc.scalar.activation(part(term_a[b], span), part(peak[b], span), ACT.Square, scale=math.sqrt(0.5))
-                engine = nc.vector if b else nc.gpsimd
-                engine.tensor_tensor(part(term_b[b], span), part(drop_abs[b], span), part(drop[b], span), ALU.mult)
 
         def turn(b):
             for n, term in enumerate((term_a[b], term_b[b])):
@@ -162,6 +160,7 @@ def tile_picked_yrus_burg_p_kernel(tc, x_words, x_scales, cT, area, qm, cur, off
         nc.gpsimd.tensor_scalar(q_bf[:], q_raw[:].rearrange("p j r -> p r j"), 1.0, 0.0, ALU.mult, ALU.add)
         for b in range(TILES):
             combine(b)
+            nc.vector.tensor_tensor(term_b[b][:], drop_abs[b][:], drop[b][:], ALU.mult)
             turn(b)
         q_codes = sbuf("q_codes", [P, R], U32, tag="left1")
         q_plane = sbuf("q_plane", [P, R], U8)

@@ -160,6 +160,18 @@ def tile_picked_yrus_burg_p_kernel(tc, x_words, x_scales, cT, area, qm, cur, off
         nc.gpsimd.tensor_scalar(q_bf[:], q_raw[:].rearrange("p j r -> p r j"), 1.0, 0.0, ALU.mult, ALU.add)
         for b in range(TILES):
             combine(b)
+            if b == 0:
+                for o, span in enumerate(halves):
+                    idle = psum.tile([P, S], F32, name=f"idle{o}", tag="state10256")
+                    nc.tensor.matmul_mx(
+                        out=idle[:],
+                        lhsT=c_codes[o][:, 0:P].bitcast(FP8X4),
+                        lhsT_scale=c_plane[o][:, 0:P],
+                        rhs=x_codes[0][1][:].bitcast(FP8X4),
+                        rhs_scale=x_plane[0][4:P, :],
+                        start=True,
+                        stop=True,
+                    )
             nc.vector.tensor_tensor(term_b[b][:], drop_abs[b][:], drop[b][:], ALU.mult)
             turn(b)
         q_codes = sbuf("q_codes", [P, R], U32, tag="left1")

@@ -48,11 +48,11 @@ def tile_picked_yrus_burg_p_kernel(tc, x_words, x_scales, cT, area, qm, cur, off
         def load_words(o):
             nc.sync.dma_start(word_win[o][:].bitcast(I32), x_words[o].rearrange("p n t -> p (n t)").bitcast(I32))
 
+        load_words(0)
         nc.sync.dma_start(lists[0][:], offs)
         nc.sync.dma_start(lists[1][:], right)
         for q in range(4):
             nc.sync.dma_start(scale_win[32 * q : 32 * q + 4 * PASSES, :].bitcast(I32), x_scales[:, 4 * q : 4 * q + 4, :].bitcast(I32))
-        load_words(0)
         for o in range(PASSES):
             nc.sync.dma_start(c_raw[o][:], c_rows[o])
         load_words(1)
@@ -68,7 +68,7 @@ def tile_picked_yrus_burg_p_kernel(tc, x_words, x_scales, cT, area, qm, cur, off
 
         x_codes = [[sbuf(f"x_codes{s}{o}", [P, S], U32, tag=f"x_codes{s}") for o in range(PASSES)] for s in range(2)]
         c_bf = [sbuf(f"c_bf{o}", [P, N, PACK], BF16) for o in range(PASSES)]
-        x_plane = [sbuf(f"x_plane{s}", [P, S], U8) for s in range(2)]
+        x_plane = [sbuf(f"x_plane{s}", [P, S], U8, tag="c_bf0" if s else None) for s in range(2)]
         c_codes = [sbuf(f"c_codes{o}", [P, N], U32) for o in range(PASSES)]
         c_plane = [sbuf(f"c_plane{o}", [P, N], U8) for o in range(PASSES)]
         HALF = S // 2
@@ -105,13 +105,12 @@ def tile_picked_yrus_burg_p_kernel(tc, x_words, x_scales, cT, area, qm, cur, off
                     product(s, o, b, span)
 
         for s in range(2):
-            nc.vector.tensor_copy(x_plane[s][:], scale_win[:].indirect(lists[s][:]))
-        for s in range(2):
             gather_words(s, 0)
         for o in range(PASSES):
             nc.scalar.copy(*weave(c_bf[o][:], c_raw[o][:]))
-            quantise(c_codes[o][:], c_plane[o][:], c_bf[o][:])
         for s in range(2):
+            nc.vector.tensor_copy(x_plane[s][:], scale_win[:].indirect(lists[s][:]))
+            quantise(c_codes[s][:], c_plane[s][:], c_bf[s][:])
             products(s, 0)
         gather_words(0, 1)
         products(0, 1)
@@ -137,7 +136,7 @@ def tile_picked_yrus_burg_p_kernel(tc, x_words, x_scales, cT, area, qm, cur, off
                 nc.scalar.copy(part(left[b], span), part(by_slot(state[0, b, 0]), span))
         flux = [psum.tile(shape, F32, name=f"flux{b}") for b in range(TILES)]
         fa_bf = [sbuf(f"fa_bf{b}", [P, P, PACK], BF16) for b in range(TILES)]
-        fa_codes = [sbuf(f"fa_codes{b}", [P, P], U32) for b in range(TILES)]
+        fa_codes = [sbuf(f"fa_codes{b}", [P, P], U32, tag=None if b else "area_sb") for b in range(TILES)]
         fa_plane = [sbuf(f"fa_plane{b}", [P, P], U8) for b in range(TILES)]
         area_wide = area_sb[:].unsqueeze(1).to_broadcast([P, P, PACK])
 
@@ -179,6 +178,7 @@ def tile_picked_yrus_burg_p_kernel(tc, x_words, x_scales, cT, area, qm, cur, off
         quantise(q_codes[:], q_plane[:], q_bf[:])
         for b in range(TILES):
             nc.vector.tensor_tensor(fa_bf[b][:], flux[b][:].rearrange("p j m -> p m j"), area_wide, ALU.mult)
+        for b in range(TILES):
             quantise(fa_codes[b][:], fa_plane[b][:], fa_bf[b][:])
         out_rows = out.rearrange("(a p) m -> p a m", p=P)
         for b in range(TILES):

@@ -50,11 +50,17 @@ def tile_picked_yrus_burg_p_kernel(tc, x_words, x_scales, cT, area, qm, cur, off
 
         load_words(0)
         nc.sync.dma_start(lists[0][:], offs)
+
+        def load_scales(rows):
+            for i in rows:
+                for o in range(PASSES):
+                    nc.sync.dma_start(scale_win[4 * o + i : P : 32, :].bitcast(I32), x_scales[o, i:16:4, :].bitcast(I32))
+
+        load_scales((0, 1))
         nc.sync.dma_start(lists[1][:], right)
-        for q in range(4):
-            nc.sync.dma_start(scale_win[32 * q : 32 * q + 4 * PASSES, :].bitcast(I32), x_scales[:, 4 * q : 4 * q + 4, :].bitcast(I32))
-        for o in range(PASSES):
-            nc.sync.dma_start(c_raw[o][:], c_rows[o])
+        nc.sync.dma_start(c_raw[0][:], c_rows[0])
+        load_scales((2, 3))
+        nc.sync.dma_start(c_raw[1][:], c_rows[1])
         load_words(1)
         q_raw = sbuf("q_raw", [P, PACK, R], F32)
         nc.sync.dma_start(q_raw[:], qm.rearrange("(p j) r -> p j r", j=PACK))

@@ -74,7 +74,7 @@ def tile_picked_yrus_burg_p_kernel(tc, x_words, x_scales, cT, area, qm, cur, off
 
         x_codes = [[sbuf(f"x_codes{s}{o}", [P, S], U32, tag=f"x_codes{s}") for o in range(PASSES)] for s in range(2)]
         c_bf = [sbuf(f"c_bf{o}", [P, N, PACK], BF16) for o in range(PASSES)]
-        x_plane = [sbuf(f"x_plane{s}", [P, S], U8, tag="c_bf0" if s else None) for s in range(2)]
+        x_plane = [sbuf(f"x_plane{s}", [P, S], U8, tag="c_raw0" if s else None) for s in range(2)]
         c_codes = [sbuf(f"c_codes{o}", [P, N], U32) for o in range(PASSES)]
         c_plane = [sbuf(f"c_plane{o}", [P, N], U8) for o in range(PASSES)]
         HALF = S // 2
@@ -142,7 +142,7 @@ def tile_picked_yrus_burg_p_kernel(tc, x_words, x_scales, cT, area, qm, cur, off
                 nc.scalar.copy(part(left[b], span), part(by_slot(state[0, b, 0]), span))
         flux = [psum.tile(shape, F32, name=f"flux{b}") for b in range(TILES)]
         fa_bf = [sbuf(f"fa_bf{b}", [P, P, PACK], BF16) for b in range(TILES)]
-        fa_codes = [sbuf(f"fa_codes{b}", [P, P], U32, tag=None if b else "area_sb") for b in range(TILES)]
+        fa_codes = [sbuf(f"fa_codes{b}", [P, P], U32, tag=None if b else "term_b1") for b in range(TILES)]
         fa_plane = [sbuf(f"fa_plane{b}", [P, P], U8) for b in range(TILES)]
         area_wide = area_sb[:].unsqueeze(1).to_broadcast([P, P, PACK])
 

@@ -80,7 +80,7 @@ def tile_picked_yrus_burg_p_kernel(tc, x_words, x_scales, cT, area, qm, cur, off
         HALF = S // 2
         whole = [slice(0, S)]
         halves = [slice(0, HALF), slice(HALF, S)]
-        spans = {(0, 0): whole, (0, 1): whole, (1, 0): halves, (1, 1): whole}
+        spans = {(s, b): halves for s in range(2) for b in range(TILES)}
         state = {
             (s, b, span.start): psum.tile([P, span.stop - span.start], F32, name=f"state{s}{b}{span.start}")
             for (s, b), cut in spans.items()
@@ -118,12 +118,11 @@ def tile_picked_yrus_burg_p_kernel(tc, x_words, x_scales, cT, area, qm, cur, off
             nc.vector.tensor_copy(x_plane[s][:], scale_win[:].indirect(lists[s][:]))
             quantise(c_codes[s][:], c_plane[s][:], c_bf[s][:])
             products(s, 0)
-        gather_words(0, 1)
-        products(0, 1)
-        for span in halves:
-            gather_words(1, 1, span)
-            product(1, 1, 0, span)
-        product(1, 1, 1, whole[0])
+        for s in range(2):
+            for span in halves:
+                gather_words(s, 1, span)
+                for b in range(TILES):
+                    product(s, 1, b, span)
 
         def by_slot(bank):
             return bank[:].rearrange("p (q j) -> p j q", j=PACK)
@@ -137,10 +136,10 @@ def tile_picked_yrus_burg_p_kernel(tc, x_words, x_scales, cT, area, qm, cur, off
         drop_abs = [sbuf(f"drop_abs{b}", shape, F32) for b in range(TILES)]
         term_a = [sbuf(f"term_a{b}", shape, F32) for b in range(TILES)]
         term_b = [sbuf(f"term_b{b}", shape, F32) for b in range(TILES)]
-        for b in range(TILES):
-            for span in spans[1, b]:
-                nc.scalar.copy(part(left[b], span), part(by_slot(state[0, b, 0]), span))
-        flux = [psum.tile(shape, F32, name=f"flux{b}") for b in range(TILES)]
+        for span in halves:
+            for b in range(TILES):
+                nc.scalar.copy(part(left[b], span), by_slot(state[0, b, span.start]))
+        flux = [psum.tile(shape, F32, name=f"flux{b}", tag=f"state0{b}0") for b in range(TILES)]
         fa_bf = [sbuf(f"fa_bf{b}", [P, P, PACK], BF16) for b in range(TILES)]
         fa_codes = [sbuf(f"fa_codes{b}", [P, P], U32, tag=None if b else "term_b1") for b in range(TILES)]
         fa_plane = [sbuf(f"fa_plane{b}", [P, P], U8) for b in range(TILES)]
@@ -148,38 +147,47 @@ def tile_picked_yrus_burg_p_kernel(tc, x_words, x_scales, cT, area, qm, cur, off
 
         peak = [sbuf(f"peak{b}", shape, F32, tag=f"peak{b}") for b in range(TILES)]
 
-        def combine(b):
-            for span in spans[1, b]:
-                other = by_slot(state[1, b, span.start])
-                nc.vector.tensor_tensor(part(drop[b], span), part(left[b], span), other, ALU.subtract)
-                nc.vector.scalar_tensor_tensor(part(peak[b], span), other, -1.0, part(left[b], span), ALU.mult, ALU.max)
-                nc.scalar.activation(part(drop_abs[b], span), part(drop[b], span), ACT.Abs, scale=0.25)
-                nc.scalar.activation(part(term_a[b], span), part(peak[b], span), ACT.Square, scale=math.sqrt(0.5))
+        def jump(b, span):
+            nc.vector.tensor_tensor(part(drop[b], span), part(left[b], span), by_slot(state[1, b, span.start]), ALU.subtract)
+            nc.scalar.activation(part(drop_abs[b], span), part(drop[b], span), ACT.Abs, scale=0.25)
+
+        def crest(b, span):
+            nc.vector.scalar_tensor_tensor(part(peak[b], span), by_slot(state[1, b, span.start]), -1.0, part(left[b], span), ALU.mult, ALU.max)
+            nc.scalar.activation(part(term_a[b], span), part(peak[b], span), ACT.Square, scale=math.sqrt(0.5))
+
+        def signed_square(engine, b, span):
+            engine.tensor_tensor(part(term_b[b], span), part(drop_abs[b], span), part(drop[b], span), ALU.mult)
 
         def turn(b):
             for n, term in enumerate((term_a[b], term_b[b])):
                 for j in range(PACK):
                     nc.tensor.matmul(flux[b][:, j, :], term[:, j, :], ident[:], start=(n, j) == (0, 0), stop=(n, j) == (1, PACK - 1), is_transpose=True)
 
-        q_bf = sbuf("q_bf", [P, R, PACK], BF16, tag="word_win1")
+        q_bf = sbuf("q_bf", [P, R, PACK], BF16)
         nc.gpsimd.tensor_scalar(q_bf[:], q_raw[:].rearrange("p j r -> p r j"), 1.0, 0.0, ALU.mult, ALU.add)
-        for b in range(TILES):
-            combine(b)
-            if b == 0:
-                for o, span in enumerate(halves):
-                    idle = psum.tile([P, S], F32, name=f"idle{o}", tag="state10256")
-                    nc.tensor.matmul_mx(
-                        out=idle[:],
-                        lhsT=c_codes[o][:, 0:P].bitcast(FP8X4),
-                        lhsT_scale=c_plane[o][:, 0:P],
-                        rhs=x_codes[0][1][:].bitcast(FP8X4),
-                        rhs_scale=x_plane[0][4:P, :],
-                        start=True,
-                        stop=True,
-                    )
-            nc.vector.tensor_tensor(term_b[b][:], drop_abs[b][:], drop[b][:], ALU.mult)
-            turn(b)
-        q_codes = sbuf("q_codes", [P, R], U32, tag="left1")
+        for span in halves:
+            jump(0, span)
+            crest(0, span)
+        signed_square(nc.gpsimd, 0, halves[0])
+        for o in range(PASSES):
+            idle = psum.tile([P, S], F32, name=f"idle{o}", tag="state10256")
+            nc.tensor.matmul_mx(
+                out=idle[:],
+                lhsT=c_codes[o][:, 0:P].bitcast(FP8X4),
+                lhsT_scale=c_plane[o][:, 0:P],
+                rhs=x_codes[0][1][:].bitcast(FP8X4),
+                rhs_scale=x_plane[0][4:P, :],
+                start=True,
+                stop=True,
+            )
+        for step in (jump, crest):
+            for span in halves:
+                step(1, span)
+        signed_square(nc.vector, 0, halves[1])
+        turn(0)
+        signed_square(nc.vector, 1, whole[0])
+        turn(1)
+        q_codes = sbuf("q_codes", [P, R], U32, tag="peak1")
         q_plane = sbuf("q_plane", [P, R], U8)
         quantise(q_codes[:], q_plane[:], q_bf[:])
         for b in range(TILES):
@@ -189,13 +197,12 @@ def tile_picked_yrus_burg_p_kernel(tc, x_words, x_scales, cT, area, qm, cur, off
         out_rows = out.rearrange("(a p) m -> p a m", p=P)
         for b in range(TILES):
             cols = slice(b * P, (b + 1) * P)
-            acc = psum.tile([P, R // P, P], F32, name=f"acc{b}", tag=f"state0{b}0")
+            acc = psum.tile([P, R // P, P], F32, name=f"acc{b}", tag=f"state0{b}{HALF}")
             for a in range(R // P):
-                rows = slice(a * P, (a + 1) * P)
                 nc.tensor.matmul_mx(
                     out=acc[:, a, :],
-                    lhsT=q_codes[:, rows].bitcast(FP8X4),
-                    lhsT_scale=q_plane[:, rows],
+                    lhsT=q_codes[:, a * P : (a + 1) * P].bitcast(FP8X4),
+                    lhsT_scale=q_plane[:, a * P : (a + 1) * P],
                     rhs=fa_codes[b][:].bitcast(FP8X4),
                     rhs_scale=fa_plane[b][:],
                     start=True,

@@ -72,26 +72,38 @@ def tile_picked_yrus_burg_p_kernel(tc, x_words, x_scales, cT, area, qm, cur, off
         ident = sbuf("ident", [P, P], F32)
         make_identity(nc, ident[:])
 
-        x_codes = [[sbuf(f"x_codes{s}{o}", [P, S], U32, tag=f"x_codes{s}") for o in range(PASSES)] for s in range(2)]
         c_bf = [sbuf(f"c_bf{o}", [P, N, PACK], BF16) for o in range(PASSES)]
+        neg_bf = sbuf("neg_bf", [P, PASSES * P, PACK], BF16)
         x_plane = [sbuf(f"x_plane{s}", [P, S], U8, tag="c_raw0" if s else None) for s in range(2)]
         c_codes = [sbuf(f"c_codes{o}", [P, N], U32) for o in range(PASSES)]
         c_plane = [sbuf(f"c_plane{o}", [P, N], U8) for o in range(PASSES)]
         HALF = S // 2
         whole = [slice(0, S)]
         halves = [slice(0, HALF), slice(HALF, S)]
-        spans = {(s, b): halves for s in range(2) for b in range(TILES)}
+        x_tiles = {
+            (s, o, span.start): sbuf(f"x_codes{s}{o}{span.start}", [P, span.stop - span.start], U32)
+            for s in range(2)
+            for o in range(PASSES)
+            for span in (halves if (s, o) == (1, 1) else whole)
+        }
+
+        def x_codes(s, o, span):
+            return x_tiles[s, o, span.start][:] if (s, o) == (1, 1) else x_tiles[s, o, 0][:, span]
+
+        late = (1, 1, HALF)
+        spans = {(s, b): halves if s else whole for s in range(2) for b in range(TILES)}
         state = {
             (s, b, span.start): psum.tile([P, span.stop - span.start], F32, name=f"state{s}{b}{span.start}")
             for (s, b), cut in spans.items()
             for span in cut
+            if (s, b, span.start) != late
         }
 
         def quantise(codes, plane, woven):
             nc.vector.quantize_mx(out=codes.bitcast(FP8X4), scales=plane, in_=woven.rearrange("p n j -> p (n j)"))
 
         def gather_words(s, o, span=whole[0]):
-            nc.vector.tensor_copy(x_codes[s][o][:, span], word_win[o][:].indirect(lists[s][:, span.start // 16 : span.stop // 16]))
+            nc.vector.tensor_copy(x_codes(s, o, span), word_win[o][:].indirect(lists[s][:, span.start // 16 : span.stop // 16]))
 
         def product(s, o, b, span):
             cols = slice(b * P, (b + 1) * P)
@@ -99,7 +111,7 @@ def tile_picked_yrus_burg_p_kernel(tc, x_words, x_scales, cT, area, qm, cur, off
                 out=state[s, b, span.start][:],
                 lhsT=c_codes[o][:, cols].bitcast(FP8X4),
                 lhsT_scale=c_plane[o][:, cols],
-                rhs=x_codes[s][o][:, span].bitcast(FP8X4),
+                rhs=x_codes(s, o, span).bitcast(FP8X4),
                 rhs_scale=x_plane[s][4 * o : P, span],
                 start=(o == 0),
                 stop=(o == PASSES - 1),
@@ -108,21 +120,25 @@ def tile_picked_yrus_burg_p_kernel(tc, x_words, x_scales, cT, area, qm, cur, off
         def products(s, o):
             for b in range(TILES):
                 for span in spans[s, b]:
-                    product(s, o, b, span)
+                    if (s, b, span.start) != late:
+                        product(s, o, b, span)
 
         for s in range(2):
             gather_words(s, 0)
         for o in range(PASSES):
             nc.scalar.copy(*weave(c_bf[o][:], c_raw[o][:]))
+        nc.gpsimd.tensor_scalar(neg_bf[:, 0:P, :], c_raw[0][:, :, P:N].rearrange("p j m -> p m j"), -1.0, 0.0, ALU.mult, ALU.add)
+        nc.gpsimd.tensor_scalar(neg_bf[:, P : 2 * P, :], c_bf[1][:, P:N, :], -1.0, 0.0, ALU.mult, ALU.add)
         for s in range(2):
             nc.vector.tensor_copy(x_plane[s][:], scale_win[:].indirect(lists[s][:]))
             quantise(c_codes[s][:], c_plane[s][:], c_bf[s][:])
             products(s, 0)
         for s in range(2):
-            for span in halves:
+            for span in spans[s, 0]:
                 gather_words(s, 1, span)
                 for b in range(TILES):
-                    product(s, 1, b, span)
+                    if (s, b, span.start) != late:
+                        product(s, 1, b, span)
 
         def by_slot(bank):
             return bank[:].rearrange("p (q j) -> p j q", j=PACK)
@@ -136,10 +152,10 @@ def tile_picked_yrus_burg_p_kernel(tc, x_words, x_scales, cT, area, qm, cur, off
         drop_abs = [sbuf(f"drop_abs{b}", shape, F32) for b in range(TILES)]
         term_a = [sbuf(f"term_a{b}", shape, F32) for b in range(TILES)]
         term_b = [sbuf(f"term_b{b}", shape, F32) for b in range(TILES)]
-        for span in halves:
-            for b in range(TILES):
-                nc.scalar.copy(part(left[b], span), by_slot(state[0, b, span.start]))
-        flux = [psum.tile(shape, F32, name=f"flux{b}", tag=f"state0{b}0") for b in range(TILES)]
+        for b in range(TILES):
+            for span in halves:
+                nc.scalar.copy(part(left[b], span), part(by_slot(state[0, b, 0]), span))
+        flux = [psum.tile(shape, F32, name=f"flux{b}") for b in range(TILES)]
         fa_bf = [sbuf(f"fa_bf{b}", [P, P, PACK], BF16) for b in range(TILES)]
         fa_codes = [sbuf(f"fa_codes{b}", [P, P], U32, tag=None if b else "term_b1") for b in range(TILES)]
         fa_plane = [sbuf(f"fa_plane{b}", [P, P], U8) for b in range(TILES)]
@@ -165,31 +181,42 @@ def tile_picked_yrus_burg_p_kernel(tc, x_words, x_scales, cT, area, qm, cur, off
 
         q_bf = sbuf("q_bf", [P, R, PACK], BF16)
         nc.gpsimd.tensor_scalar(q_bf[:], q_raw[:].rearrange("p j r -> p r j"), 1.0, 0.0, ALU.mult, ALU.add)
-        for span in halves:
-            jump(0, span)
-            crest(0, span)
-        signed_square(nc.gpsimd, 0, halves[0])
+        jump(0, halves[0])
+        crest(0, halves[0])
+        state[late] = psum.tile([P, HALF], F32, name="state_late", tag="state100")
         for o in range(PASSES):
-            idle = psum.tile([P, S], F32, name=f"idle{o}", tag="state10256")
-            nc.tensor.matmul_mx(
-                out=idle[:],
-                lhsT=c_codes[o][:, 0:P].bitcast(FP8X4),
-                lhsT_scale=c_plane[o][:, 0:P],
-                rhs=x_codes[0][1][:].bitcast(FP8X4),
-                rhs_scale=x_plane[0][4:P, :],
-                start=True,
-                stop=True,
-            )
-        for step in (jump, crest):
-            for span in halves:
-                step(1, span)
+            product(1, o, 1, halves[1])
+        neg_codes = sbuf("neg_codes", [P, PASSES * P], U32, tag="x_codes110")
+        neg_plane = sbuf("neg_plane", [P, PASSES * P], U8)
+        quantise(neg_codes[:], neg_plane[:], neg_bf[:])
+        jump(0, halves[1])
+        crest(0, halves[1])
+        signed_square(nc.gpsimd, 0, halves[0])
+        last = halves[1]
+        last_drop = psum.tile([P, HALF], F32, name="last_drop", tag="state10256")
+        for s in range(2):
+            for o in range(PASSES):
+                nc.tensor.matmul_mx(
+                    out=last_drop[:],
+                    lhsT=(neg_codes[:, o * P : (o + 1) * P] if s else c_codes[o][:, P:N]).bitcast(FP8X4),
+                    lhsT_scale=neg_plane[:, o * P : (o + 1) * P] if s else c_plane[o][:, P:N],
+                    rhs=x_codes(s, o, last).bitcast(FP8X4),
+                    rhs_scale=x_plane[s][4 * o : P, last],
+                    start=(s, o) == (0, 0),
+                    stop=(s, o) == (1, PASSES - 1),
+                )
+        jump(1, halves[0])
+        crest(1, halves[0])
+        nc.scalar.activation(part(drop_abs[1], last), by_slot(last_drop), ACT.Abs, scale=0.25)
+        crest(1, halves[1])
         signed_square(nc.vector, 0, halves[1])
         turn(0)
-        signed_square(nc.vector, 1, whole[0])
-        turn(1)
-        q_codes = sbuf("q_codes", [P, R], U32, tag="peak1")
+        signed_square(nc.vector, 1, halves[0])
+        q_codes = sbuf("q_codes", [P, R], U32, tag="left1")
         q_plane = sbuf("q_plane", [P, R], U8)
         quantise(q_codes[:], q_plane[:], q_bf[:])
+        nc.vector.tensor_tensor(part(term_b[1], last), part(drop_abs[1], last), by_slot(last_drop), ALU.mult)
+        turn(1)
         for b in range(TILES):
             nc.vector.tensor_tensor(fa_bf[b][:], flux[b][:].rearrange("p j m -> p m j"), area_wide, ALU.mult)
         for b in range(TILES):
@@ -197,7 +224,7 @@ def tile_picked_yrus_burg_p_kernel(tc, x_words, x_scales, cT, area, qm, cur, off
         out_rows = out.rearrange("(a p) m -> p a m", p=P)
         for b in range(TILES):
             cols = slice(b * P, (b + 1) * P)
-            acc = psum.tile([P, R // P, P], F32, name=f"acc{b}", tag=f"state0{b}{HALF}")
+            acc = psum.tile([P, R // P, P], F32, name=f"acc{b}", tag=f"state0{b}0")
             for a in range(R // P):
                 nc.tensor.matmul_mx(
                     out=acc[:, a, :],

@@ -127,8 +127,8 @@ def tile_picked_yrus_burg_p_kernel(tc, x_words, x_scales, cT, area, qm, cur, off
             gather_words(s, 0)
         for o in range(PASSES):
             nc.scalar.copy(*weave(c_bf[o][:], c_raw[o][:]))
-        nc.gpsimd.tensor_scalar(neg_bf[:, 0:P, :], c_raw[0][:, :, P:N].rearrange("p j m -> p m j"), -1.0, 0.0, ALU.mult, ALU.add)
-        nc.gpsimd.tensor_scalar(neg_bf[:, P : 2 * P, :], c_bf[1][:, P:N, :], -1.0, 0.0, ALU.mult, ALU.add)
+        for o in range(PASSES):
+            nc.scalar.activation(neg_bf[:, o * P : (o + 1) * P, :], c_bf[o][:, P:N, :], ACT.Copy, scale=-1.0)
         for s in range(2):
             nc.vector.tensor_copy(x_plane[s][:], scale_win[:].indirect(lists[s][:]))
             quantise(c_codes[s][:], c_plane[s][:], c_bf[s][:])

@@ -179,8 +179,8 @@ def tile_picked_yrus_burg_p_kernel(tc, x_words, x_scales, cT, area, qm, cur, off
                 for j in range(PACK):
                     nc.tensor.matmul(flux[b][:, j, :], term[:, j, :], ident[:], start=(n, j) == (0, 0), stop=(n, j) == (1, PACK - 1), is_transpose=True)
 
-        q_bf = sbuf("q_bf", [P, R, PACK], BF16)
-        nc.gpsimd.tensor_scalar(q_bf[:], q_raw[:].rearrange("p j r -> p r j"), 1.0, 0.0, ALU.mult, ALU.add)
+        q_bf = [sbuf("q_bf0", [P, P, PACK], BF16)]
+        nc.gpsimd.tensor_scalar(q_bf[0][:], q_raw[:, :, 0:P].rearrange("p j r -> p r j"), 1.0, 0.0, ALU.mult, ALU.add)
         jump(0, halves[0])
         crest(0, halves[0])
         state[late] = psum.tile([P, HALF], F32, name="state_late", tag="state100")
@@ -209,16 +209,21 @@ def tile_picked_yrus_burg_p_kernel(tc, x_words, x_scales, cT, area, qm, cur, off
         crest(1, halves[0])
         nc.scalar.activation(part(drop_abs[1], last), by_slot(last_drop), ACT.Abs, scale=0.25)
         crest(1, halves[1])
+        q_bf.append(sbuf("q_bf1", [P, P, PACK], BF16, tag="x_codes110"))
+        nc.scalar.copy(*weave(q_bf[1][:], q_raw[:, :, P:R]))
         signed_square(nc.vector, 0, halves[1])
         turn(0)
         signed_square(nc.vector, 1, halves[0])
-        q_codes = sbuf("q_codes", [P, R], U32, tag="left1")
-        q_plane = sbuf("q_plane", [P, R], U8)
-        quantise(q_codes[:], q_plane[:], q_bf[:])
+        q_codes = [sbuf("q_codes0", [P, P], U32, tag="left1")]
+        q_plane = [sbuf(f"q_plane{a}", [P, P], U8) for a in range(R // P)]
+        quantise(q_codes[0][:], q_plane[0][:], q_bf[0][:])
         nc.vector.tensor_tensor(part(term_b[1], last), part(drop_abs[1], last), by_slot(last_drop), ALU.mult)
         turn(1)
+        q_codes.append(sbuf("q_codes1", [P, P], U32, tag="term_a1"))
         for b in range(TILES):
             nc.vector.tensor_tensor(fa_bf[b][:], flux[b][:].rearrange("p j m -> p m j"), area_wide, ALU.mult)
+            if b == 0:
+                quantise(q_codes[1][:], q_plane[1][:], q_bf[1][:])
         for b in range(TILES):
             quantise(fa_codes[b][:], fa_plane[b][:], fa_bf[b][:])
         out_rows = out.rearrange("(a p) m -> p a m", p=P)
@@ -228,8 +233,8 @@ def tile_picked_yrus_burg_p_kernel(tc, x_words, x_scales, cT, area, qm, cur, off
             for a in range(R // P):
                 nc.tensor.matmul_mx(
                     out=acc[:, a, :],
-                    lhsT=q_codes[:, a * P : (a + 1) * P].bitcast(FP8X4),
-                    lhsT_scale=q_plane[:, a * P : (a + 1) * P],
+                    lhsT=q_codes[a][:].bitcast(FP8X4),
+                    lhsT_scale=q_plane[a][:],
                     rhs=fa_codes[b][:].bitcast(FP8X4),
                     rhs_scale=fa_plane[b][:],
                     start=True,

@@ -38,43 +38,44 @@ def tile_picked_yrus_burg_p_kernel(tc, x_words, x_scales, cT, area, qm, cur, off
 
         lists = [keep.tile([P, S // 16], U16, name=f"list{s}") for s in range(2)]
 
+        ROWS = PASSES * 16
         scale_win = sbuf("scale_win", [P, T], U8)
-        nc.gpsimd.memset(scale_win[:].bitcast(I32), 0)
+        nc.vector.memset(scale_win[2 * ROWS : P, :].bitcast(I32), 0)
+        nc.gpsimd.memset(scale_win[ROWS : 2 * ROWS, :].bitcast(I32), 0)
+        x_plane = [sbuf(f"x_plane{o}", [P, 2 * S], U8) for o in range(PASSES)]
+        for o in range(PASSES):
+            nc.gpsimd.memset(x_plane[o][:].bitcast(I32), 0)
 
         word_win = [sbuf(f"word_win{o}", [P, T], U32) for o in range(PASSES)]
-        c_raw = [sbuf(f"c_raw{o}", [P, PACK, N], F32) for o in range(PASSES)]
+        c_raw = [sbuf("c_raw0", [P, PACK, N], F32)]
         c_rows = cT.rearrange("(o p j) m -> o p j m", o=PASSES, j=PACK)
 
         def load_words(o):
             nc.sync.dma_start(word_win[o][:].bitcast(I32), x_words[o].rearrange("p n t -> p (n t)").bitcast(I32))
 
-        load_words(0)
+        nc.sync.dma_start(scale_win[0:ROWS, :].bitcast(I32), x_scales.rearrange("o q t -> (o q) t").bitcast(I32))
         nc.sync.dma_start(lists[0][:], offs)
-
-        def load_scales(rows):
-            for i in rows:
-                for o in range(PASSES):
-                    nc.sync.dma_start(scale_win[4 * o + i : P : 32, :].bitcast(I32), x_scales[o, i:16:4, :].bitcast(I32))
-
-        load_scales((0, 1))
         nc.sync.dma_start(lists[1][:], right)
+        load_words(0)
         nc.sync.dma_start(c_raw[0][:], c_rows[0])
-        load_scales((2, 3))
-        nc.sync.dma_start(c_raw[1][:], c_rows[1])
         load_words(1)
-        q_raw = sbuf("q_raw", [P, PACK, R], F32)
-        nc.sync.dma_start(q_raw[:], qm.rearrange("(p j) r -> p j r", j=PACK))
-        area_sb = sbuf("area_sb", [P, PACK], F32)
-        nc.sync.dma_start(area_sb[:], area.rearrange("(p j) o -> p (j o)", j=PACK))
-        cur_sb = sbuf("cur_sb", [P, R // P, N], F32)
-        nc.sync.dma_start(cur_sb[:], cur.rearrange("(a p) m -> p a m", p=P))
+        picked = sbuf("picked", [P, 2 * S], U8)
+        for s in range(2):
+            nc.vector.tensor_copy(picked[:, s * S : (s + 1) * S], scale_win[:].indirect(lists[s][:]))
 
+        def relay(o):
+            for quad in range(4):
+                nc.sync.dma_start(x_plane[o][32 * quad : 32 * quad + 4, :].bitcast(I32), picked[16 * o + 4 * quad : 16 * o + 4 * quad + 4, :].bitcast(I32))
+
+        relay(0)
+        c_raw.append(sbuf("c_raw1", [P, PACK, N], F32, tag="scale_win"))
+        nc.sync.dma_start(c_raw[1][:], c_rows[1])
+        relay(1)
         ident = sbuf("ident", [P, P], F32)
         make_identity(nc, ident[:])
 
         c_bf = [sbuf(f"c_bf{o}", [P, N, PACK], BF16) for o in range(PASSES)]
         neg_bf = sbuf("neg_bf", [P, PASSES * P, PACK], BF16)
-        x_plane = [sbuf(f"x_plane{s}", [P, S], U8, tag="c_raw0" if s else None) for s in range(2)]
         c_codes = [sbuf(f"c_codes{o}", [P, N], U32) for o in range(PASSES)]
         c_plane = [sbuf(f"c_plane{o}", [P, N], U8) for o in range(PASSES)]
         HALF = S // 2
@@ -85,6 +86,7 @@ def tile_picked_yrus_burg_p_kernel(tc, x_words, x_scales, cT, area, qm, cur, off
             for s in range(2)
             for o in range(PASSES)
             for span in (halves if (s, o) == (1, 1) else whole)
+            if (s, o, span.start) not in ((1, 1, HALF), (0, 1, 0))
         }
 
         def x_codes(s, o, span):
@@ -112,7 +114,7 @@ def tile_picked_yrus_burg_p_kernel(tc, x_words, x_scales, cT, area, qm, cur, off
                 lhsT=c_codes[o][:, cols].bitcast(FP8X4),
                 lhsT_scale=c_plane[o][:, cols],
                 rhs=x_codes(s, o, span).bitcast(FP8X4),
-                rhs_scale=x_plane[s][4 * o : P, span],
+                rhs_scale=x_plane[o][:, s * S + span.start : s * S + span.stop],
                 start=(o == 0),
                 stop=(o == PASSES - 1),
             )
@@ -125,18 +127,31 @@ def tile_picked_yrus_burg_p_kernel(tc, x_words, x_scales, cT, area, qm, cur, off
 
         for s in range(2):
             gather_words(s, 0)
-        for o in range(PASSES):
-            nc.scalar.copy(*weave(c_bf[o][:], c_raw[o][:]))
-        for o in range(PASSES):
-            nc.scalar.activation(neg_bf[:, o * P : (o + 1) * P, :], c_bf[o][:, P:N, :], ACT.Copy, scale=-1.0)
+        nc.scalar.copy(*weave(c_bf[0][:], c_raw[0][:]))
+        nc.scalar.activation(neg_bf[:, 0:P, :], c_bf[0][:, P:N, :], ACT.Copy, scale=-1.0)
+        quantise(c_codes[0][:], c_plane[0][:], c_bf[0][:])
+        q_raw = sbuf("q_raw", [P, PACK, R], F32, tag="word_win0")
+        nc.sync.dma_start(q_raw[:], qm.rearrange("(p j) r -> p j r", j=PACK))
+        area_sb = sbuf("area_sb", [P, PACK], F32, tag="c_bf0")
+        nc.sync.dma_start(area_sb[:], area.rearrange("(p j) o -> p (j o)", j=PACK))
+        cur_sb = sbuf("cur_sb", [P, R // P, N], F32, tag="picked")
+        nc.sync.dma_start(cur_sb[:], cur.rearrange("(a p) m -> p a m", p=P))
+
         for s in range(2):
-            nc.vector.tensor_copy(x_plane[s][:], scale_win[:].indirect(lists[s][:]))
-            quantise(c_codes[s][:], c_plane[s][:], c_bf[s][:])
             products(s, 0)
-        for s in range(2):
-            for span in spans[s, 0]:
-                gather_words(s, 1, span)
-                for b in range(TILES):
+        nc.scalar.copy(*weave(c_bf[1][:, 0:P, :], c_raw[1][:, :, 0:P]))
+        nc.gpsimd.tensor_scalar(c_bf[1][:, P:N, :], c_raw[1][:, :, P:N].rearrange("p j r -> p r j"), 1.0, 0.0, ALU.mult, ALU.add)
+        nc.scalar.activation(neg_bf[:, P : 2 * P, :], c_bf[1][:, P:N, :], ACT.Copy, scale=-1.0)
+        x_tiles[0, 1, 0] = sbuf("x_codes010", [P, S], U32, tag="c_raw0")
+        gather_words(0, 1)
+        gather_words(1, 1, halves[0])
+        quantise(c_codes[1][:, 0:P], c_plane[1][:, 0:P], c_bf[1][:, 0:P, :])
+        x_tiles[1, 1, HALF] = sbuf("x_codes11last", [P, HALF], U32, tag="scale_win")
+        gather_words(1, 1, halves[1])
+        quantise(c_codes[1][:, P:N], c_plane[1][:, P:N], c_bf[1][:, P:N, :])
+        for b in range(TILES):
+            for s in range(2):
+                for span in spans[s, b]:
                     if (s, b, span.start) != late:
                         product(s, 1, b, span)
 
@@ -179,16 +194,16 @@ def tile_picked_yrus_burg_p_kernel(tc, x_words, x_scales, cT, area, qm, cur, off
                 for j in range(PACK):
                     nc.tensor.matmul(flux[b][:, j, :], term[:, j, :], ident[:], start=(n, j) == (0, 0), stop=(n, j) == (1, PACK - 1), is_transpose=True)
 
-        q_bf = [sbuf("q_bf0", [P, P, PACK], BF16)]
+        neg_codes = sbuf("neg_codes", [P, PASSES * P], U32)
+        neg_plane = sbuf("neg_plane", [P, PASSES * P], U8)
+        quantise(neg_codes[:], neg_plane[:], neg_bf[:])
+        q_bf = [sbuf("q_bf0", [P, P, PACK], BF16, tag="neg_bf")]
         nc.gpsimd.tensor_scalar(q_bf[0][:], q_raw[:, :, 0:P].rearrange("p j r -> p r j"), 1.0, 0.0, ALU.mult, ALU.add)
         jump(0, halves[0])
         crest(0, halves[0])
         state[late] = psum.tile([P, HALF], F32, name="state_late", tag="state100")
         for o in range(PASSES):
             product(1, o, 1, halves[1])
-        neg_codes = sbuf("neg_codes", [P, PASSES * P], U32, tag="x_codes110")
-        neg_plane = sbuf("neg_plane", [P, PASSES * P], U8)
-        quantise(neg_codes[:], neg_plane[:], neg_bf[:])
         jump(0, halves[1])
         crest(0, halves[1])
         signed_square(nc.gpsimd, 0, halves[0])
@@ -201,7 +216,7 @@ def tile_picked_yrus_burg_p_kernel(tc, x_words, x_scales, cT, area, qm, cur, off
                     lhsT=(neg_codes[:, o * P : (o + 1) * P] if s else c_codes[o][:, P:N]).bitcast(FP8X4),
                     lhsT_scale=neg_plane[:, o * P : (o + 1) * P] if s else c_plane[o][:, P:N],
                     rhs=x_codes(s, o, last).bitcast(FP8X4),
-                    rhs_scale=x_plane[s][4 * o : P, last],
+                    rhs_scale=x_plane[o][:, s * S + last.start : s * S + last.stop],
                     start=(s, o) == (0, 0),
                     stop=(s, o) == (1, PASSES - 1),
                 )

@@ -86,7 +86,7 @@ def tile_picked_yrus_burg_p_kernel(tc, x_words, x_scales, cT, area, qm, cur, off
             for s in range(2)
             for o in range(PASSES)
             for span in (halves if (s, o) == (1, 1) else whole)
-            if (s, o, span.start) not in ((1, 1, HALF), (0, 1, 0))
+            if (s, o, span.start) not in ((1, 1, HALF), (0, 1, 0), (1, 1, 0))
         }
 
         def x_codes(s, o, span):
@@ -142,7 +142,9 @@ def tile_picked_yrus_burg_p_kernel(tc, x_words, x_scales, cT, area, qm, cur, off
         nc.scalar.copy(*weave(c_bf[1][:, 0:P, :], c_raw[1][:, :, 0:P]))
         nc.gpsimd.tensor_scalar(c_bf[1][:, P:N, :], c_raw[1][:, :, P:N].rearrange("p j r -> p r j"), 1.0, 0.0, ALU.mult, ALU.add)
         nc.scalar.activation(neg_bf[:, P : 2 * P, :], c_bf[1][:, P:N, :], ACT.Copy, scale=-1.0)
-        x_tiles[0, 1, 0] = sbuf("x_codes010", [P, S], U32, tag="c_raw0")
+        held = sbuf("x_codes_held", [P, S + HALF], U32, tag="c_raw0")
+        x_tiles[0, 1, 0] = held[:, 0:S]
+        x_tiles[1, 1, 0] = held[:, S : S + HALF]
         gather_words(0, 1)
         gather_words(1, 1, halves[0])
         quantise(c_codes[1][:, 0:P], c_plane[1][:, 0:P], c_bf[1][:, 0:P, :])
@@ -224,7 +226,7 @@ def tile_picked_yrus_burg_p_kernel(tc, x_words, x_scales, cT, area, qm, cur, off
         crest(1, halves[0])
         nc.scalar.activation(part(drop_abs[1], last), by_slot(last_drop), ACT.Abs, scale=0.25)
         crest(1, halves[1])
-        q_bf.append(sbuf("q_bf1", [P, P, PACK], BF16, tag="x_codes110"))
+        q_bf.append(sbuf("q_bf1", [P, P, PACK], BF16, tag="neg_codes"))
         nc.scalar.copy(*weave(q_bf[1][:], q_raw[:, :, P:R]))
         signed_square(nc.vector, 0, halves[1])
         turn(0)

@@ -65,7 +65,8 @@ def tile_picked_yrus_burg_p_kernel(tc, x_words, x_scales, cT, area, qm, cur, off
 
         def relay(o):
             for quad in range(4):
-                nc.sync.dma_start(x_plane[o][32 * quad : 32 * quad + 4, :].bitcast(I32), picked[16 * o + 4 * quad : 16 * o + 4 * quad + 4, :].bitcast(I32))
+                queue = nc.gpsimd if o == 1 and quad >= 2 else nc.sync
+                queue.dma_start(x_plane[o][32 * quad : 32 * quad + 4, :].bitcast(I32), picked[16 * o + 4 * quad : 16 * o + 4 * quad + 4, :].bitcast(I32))
 
         relay(0)
         c_raw.append(sbuf("c_raw1", [P, PACK, N], F32, tag="scale_win"))
@@ -74,8 +75,11 @@ def tile_picked_yrus_burg_p_kernel(tc, x_words, x_scales, cT, area, qm, cur, off
         ident = sbuf("ident", [P, P], F32)
         make_identity(nc, ident[:])
 
-        c_bf = [sbuf(f"c_bf{o}", [P, N, PACK], BF16) for o in range(PASSES)]
-        neg_bf = sbuf("neg_bf", [P, PASSES * P, PACK], BF16)
+        c_bf = [sbuf("c_bf0", [P, N, PACK], BF16)]
+        c_last = [sbuf(f"c_last{b}", [P, P, PACK], BF16) for b in range(TILES)]
+        neg_bf = [sbuf(f"neg_bf{o}", [P, P, PACK], BF16) for o in range(PASSES)]
+        neg_codes = [sbuf(f"neg_codes{o}", [P, P], U32) for o in range(PASSES)]
+        neg_plane = [sbuf(f"neg_plane{o}", [P, P], U8) for o in range(PASSES)]
         c_codes = [sbuf(f"c_codes{o}", [P, N], U32) for o in range(PASSES)]
         c_plane = [sbuf(f"c_plane{o}", [P, N], U8) for o in range(PASSES)]
         HALF = S // 2
@@ -93,7 +97,7 @@ def tile_picked_yrus_burg_p_kernel(tc, x_words, x_scales, cT, area, qm, cur, off
             return x_tiles[s, o, span.start][:] if (s, o) == (1, 1) else x_tiles[s, o, 0][:, span]
 
         late = (1, 1, HALF)
-        spans = {(s, b): halves if s else whole for s in range(2) for b in range(TILES)}
+        spans = {(s, b): whole if (s, b) == (0, 1) else halves for s in range(2) for b in range(TILES)}
         state = {
             (s, b, span.start): psum.tile([P, span.stop - span.start], F32, name=f"state{s}{b}{span.start}")
             for (s, b), cut in spans.items()
@@ -128,34 +132,36 @@ def tile_picked_yrus_burg_p_kernel(tc, x_words, x_scales, cT, area, qm, cur, off
         for s in range(2):
             gather_words(s, 0)
         nc.scalar.copy(*weave(c_bf[0][:], c_raw[0][:]))
-        nc.scalar.activation(neg_bf[:, 0:P, :], c_bf[0][:, P:N, :], ACT.Copy, scale=-1.0)
+        nc.scalar.activation(neg_bf[0][:], c_bf[0][:, P:N, :], ACT.Copy, scale=-1.0)
         quantise(c_codes[0][:], c_plane[0][:], c_bf[0][:])
+        quantise(neg_codes[0][:], neg_plane[0][:], neg_bf[0][:])
         q_raw = sbuf("q_raw", [P, PACK, R], F32, tag="word_win0")
         nc.sync.dma_start(q_raw[:], qm.rearrange("(p j) r -> p j r", j=PACK))
         area_sb = sbuf("area_sb", [P, PACK], F32, tag="c_bf0")
         nc.sync.dma_start(area_sb[:], area.rearrange("(p j) o -> p (j o)", j=PACK))
-        cur_sb = sbuf("cur_sb", [P, R // P, N], F32, tag="picked")
-        nc.sync.dma_start(cur_sb[:], cur.rearrange("(a p) m -> p a m", p=P))
 
         for s in range(2):
             products(s, 0)
-        nc.scalar.copy(*weave(c_bf[1][:, 0:P, :], c_raw[1][:, :, 0:P]))
-        nc.gpsimd.tensor_scalar(c_bf[1][:, P:N, :], c_raw[1][:, :, P:N].rearrange("p j r -> p r j"), 1.0, 0.0, ALU.mult, ALU.add)
-        nc.scalar.activation(neg_bf[:, P : 2 * P, :], c_bf[1][:, P:N, :], ACT.Copy, scale=-1.0)
+        cur_sb = sbuf("cur_sb", [P, R // P, N], F32, tag="x_codes000")
+        nc.sync.dma_start(cur_sb[:], cur.rearrange("(a p) m -> p a m", p=P))
+        nc.scalar.copy(*weave(c_last[0][:, 0:64, :], c_raw[1][:, :, 0:64]))
+        nc.gpsimd.tensor_scalar(c_last[0][:, 64:P, :], c_raw[1][:, :, 64:P].rearrange("p j r -> p r j"), 1.0, 0.0, ALU.mult, ALU.add)
+        nc.scalar.copy(*weave(c_last[1][:], c_raw[1][:, :, P:N]))
+        nc.scalar.activation(neg_bf[1][:], c_last[1][:], ACT.Copy, scale=-1.0)
         held = sbuf("x_codes_held", [P, S + HALF], U32, tag="c_raw0")
         x_tiles[0, 1, 0] = held[:, 0:S]
         x_tiles[1, 1, 0] = held[:, S : S + HALF]
         gather_words(0, 1)
         gather_words(1, 1, halves[0])
-        quantise(c_codes[1][:, 0:P], c_plane[1][:, 0:P], c_bf[1][:, 0:P, :])
-        x_tiles[1, 1, HALF] = sbuf("x_codes11last", [P, HALF], U32, tag="scale_win")
+        quantise(c_codes[1][:, 0:P], c_plane[1][:, 0:P], c_last[0][:])
+        x_tiles[1, 1, HALF] = sbuf("x_codes11last", [P, HALF], U32, tag="c_last0")
         gather_words(1, 1, halves[1])
-        quantise(c_codes[1][:, P:N], c_plane[1][:, P:N], c_bf[1][:, P:N, :])
-        for b in range(TILES):
+        quantise(c_codes[1][:, P:N], c_plane[1][:, P:N], c_last[1][:])
+        for span in halves:
             for s in range(2):
-                for span in spans[s, b]:
-                    if (s, b, span.start) != late:
-                        product(s, 1, b, span)
+                product(s, 1, 0, span)
+        product(0, 1, 1, whole[0])
+        product(1, 1, 1, halves[0])
 
         def by_slot(bank):
             return bank[:].rearrange("p (q j) -> p j q", j=PACK)
@@ -169,9 +175,10 @@ def tile_picked_yrus_burg_p_kernel(tc, x_words, x_scales, cT, area, qm, cur, off
         drop_abs = [sbuf(f"drop_abs{b}", shape, F32) for b in range(TILES)]
         term_a = [sbuf(f"term_a{b}", shape, F32) for b in range(TILES)]
         term_b = [sbuf(f"term_b{b}", shape, F32) for b in range(TILES)]
-        for b in range(TILES):
-            for span in halves:
-                nc.scalar.copy(part(left[b], span), part(by_slot(state[0, b, 0]), span))
+        for span in halves:
+            nc.scalar.copy(part(left[0], span), by_slot(state[0, 0, span.start]))
+        for span in halves:
+            nc.scalar.copy(part(left[1], span), part(by_slot(state[0, 1, 0]), span))
         flux = [psum.tile(shape, F32, name=f"flux{b}") for b in range(TILES)]
         fa_bf = [sbuf(f"fa_bf{b}", [P, P, PACK], BF16) for b in range(TILES)]
         fa_codes = [sbuf(f"fa_codes{b}", [P, P], U32, tag=None if b else "term_b1") for b in range(TILES)]
@@ -196,10 +203,8 @@ def tile_picked_yrus_burg_p_kernel(tc, x_words, x_scales, cT, area, qm, cur, off
                 for j in range(PACK):
                     nc.tensor.matmul(flux[b][:, j, :], term[:, j, :], ident[:], start=(n, j) == (0, 0), stop=(n, j) == (1, PACK - 1), is_transpose=True)
 
-        neg_codes = sbuf("neg_codes", [P, PASSES * P], U32)
-        neg_plane = sbuf("neg_plane", [P, PASSES * P], U8)
-        quantise(neg_codes[:], neg_plane[:], neg_bf[:])
-        q_bf = [sbuf("q_bf0", [P, P, PACK], BF16, tag="neg_bf")]
+        quantise(neg_codes[1][:], neg_plane[1][:], neg_bf[1][:])
+        q_bf = [sbuf("q_bf0", [P, P, PACK], BF16, tag="neg_bf1")]
         nc.gpsimd.tensor_scalar(q_bf[0][:], q_raw[:, :, 0:P].rearrange("p j r -> p r j"), 1.0, 0.0, ALU.mult, ALU.add)
         jump(0, halves[0])
         crest(0, halves[0])
@@ -215,8 +220,8 @@ def tile_picked_yrus_burg_p_kernel(tc, x_words, x_scales, cT, area, qm, cur, off
             for o in range(PASSES):
                 nc.tensor.matmul_mx(
                     out=last_drop[:],
-                    lhsT=(neg_codes[:, o * P : (o + 1) * P] if s else c_codes[o][:, P:N]).bitcast(FP8X4),
-                    lhsT_scale=neg_plane[:, o * P : (o + 1) * P] if s else c_plane[o][:, P:N],
+                    lhsT=(neg_codes[o][:] if s else c_codes[o][:, P:N]).bitcast(FP8X4),
+                    lhsT_scale=neg_plane[o][:] if s else c_plane[o][:, P:N],
                     rhs=x_codes(s, o, last).bitcast(FP8X4),
                     rhs_scale=x_plane[o][:, s * S + last.start : s * S + last.stop],
                     start=(s, o) == (0, 0),
@@ -226,7 +231,7 @@ def tile_picked_yrus_burg_p_kernel(tc, x_words, x_scales, cT, area, qm, cur, off
         crest(1, halves[0])
         nc.scalar.activation(part(drop_abs[1], last), by_slot(last_drop), ACT.Abs, scale=0.25)
         crest(1, halves[1])
-        q_bf.append(sbuf("q_bf1", [P, P, PACK], BF16, tag="neg_codes"))
+        q_bf.append(sbuf("q_bf1", [P, P, PACK], BF16, tag="neg_codes1"))
         nc.scalar.copy(*weave(q_bf[1][:], q_raw[:, :, P:R]))
         signed_square(nc.vector, 0, halves[1])
         turn(0)

@@ -43,8 +43,7 @@ def tile_picked_yrus_burg_p_kernel(tc, x_words, x_scales, cT, area, qm, cur, off
         nc.vector.memset(scale_win[2 * ROWS : P, :].bitcast(I32), 0)
         nc.gpsimd.memset(scale_win[ROWS : 2 * ROWS, :].bitcast(I32), 0)
         x_plane = [sbuf(f"x_plane{o}", [P, 2 * S], U8) for o in range(PASSES)]
-        for o in range(PASSES):
-            nc.gpsimd.memset(x_plane[o][:].bitcast(I32), 0)
+        nc.gpsimd.memset(x_plane[1][:].bitcast(I32), 0)
 
         word_win = [sbuf(f"word_win{o}", [P, T], U32) for o in range(PASSES)]
         c_raw = [sbuf("c_raw0", [P, PACK, N], F32)]
@@ -64,10 +63,10 @@ def tile_picked_yrus_burg_p_kernel(tc, x_words, x_scales, cT, area, qm, cur, off
             nc.vector.tensor_copy(picked[:, s * S : (s + 1) * S], scale_win[:].indirect(lists[s][:]))
 
         def relay(o):
-            for quad in range(4):
-                queue = nc.gpsimd if o == 1 and quad >= 2 else nc.sync
-                queue.dma_start(x_plane[o][32 * quad : 32 * quad + 4, :].bitcast(I32), picked[16 * o + 4 * quad : 16 * o + 4 * quad + 4, :].bitcast(I32))
+            for quad in range(1 - o, 4):
+                nc.sync.dma_start(x_plane[o][32 * quad : 32 * quad + 4, :].bitcast(I32), picked[16 * o + 4 * quad : 16 * o + 4 * quad + 4, :].bitcast(I32))
 
+        nc.vector.tensor_copy(x_plane[0][:].bitcast(I32), picked[:].bitcast(I32))
         relay(0)
         c_raw.append(sbuf("c_raw1", [P, PACK, N], F32, tag="scale_win"))
         nc.sync.dma_start(c_raw[1][:], c_rows[1])

@@ -43,10 +43,11 @@ def tile_picked_yrus_burg_p_kernel(tc, x_words, x_scales, cT, area, qm, cur, off
         nc.vector.memset(scale_win[2 * ROWS : P, :].bitcast(I32), 0)
         nc.gpsimd.memset(scale_win[ROWS : 2 * ROWS, :].bitcast(I32), 0)
         x_plane = [sbuf(f"x_plane{o}", [P, 2 * S], U8) for o in range(PASSES)]
-        nc.gpsimd.memset(x_plane[1][:].bitcast(I32), 0)
+        for o in range(PASSES):
+            nc.gpsimd.memset(x_plane[o][:].bitcast(I32), 0)
 
-        word_win = [sbuf(f"word_win{o}", [P, T], U32) for o in range(PASSES)]
-        c_raw = [sbuf("c_raw0", [P, PACK, N], F32)]
+        word_win = [sbuf("word_win0", [P, T], U32)]
+        c_raw = [sbuf(f"c_raw{o}", [P, PACK, N], F32) for o in range(PASSES)]
         c_rows = cT.rearrange("(o p j) m -> o p j m", o=PASSES, j=PACK)
 
         def load_words(o):
@@ -56,29 +57,30 @@ def tile_picked_yrus_burg_p_kernel(tc, x_words, x_scales, cT, area, qm, cur, off
         nc.sync.dma_start(lists[0][:], offs)
         nc.sync.dma_start(lists[1][:], right)
         load_words(0)
-        nc.sync.dma_start(c_raw[0][:], c_rows[0])
-        load_words(1)
+        for o in range(PASSES):
+            nc.sync.dma_start(c_raw[o][:], c_rows[o])
         picked = sbuf("picked", [P, 2 * S], U8)
         for s in range(2):
             nc.vector.tensor_copy(picked[:, s * S : (s + 1) * S], scale_win[:].indirect(lists[s][:]))
 
         def relay(o):
-            for quad in range(1 - o, 4):
+            for quad in range(4):
                 nc.sync.dma_start(x_plane[o][32 * quad : 32 * quad + 4, :].bitcast(I32), picked[16 * o + 4 * quad : 16 * o + 4 * quad + 4, :].bitcast(I32))
 
-        nc.vector.tensor_copy(x_plane[0][:].bitcast(I32), picked[:].bitcast(I32))
         relay(0)
-        c_raw.append(sbuf("c_raw1", [P, PACK, N], F32, tag="scale_win"))
-        nc.sync.dma_start(c_raw[1][:], c_rows[1])
+        word_win.append(sbuf("word_win1", [P, T], U32, tag="scale_win"))
+        load_words(1)
         relay(1)
         ident = sbuf("ident", [P, P], F32)
         make_identity(nc, ident[:])
 
-        c_bf = [sbuf("c_bf0", [P, N, PACK], BF16)]
-        c_last = [sbuf(f"c_last{b}", [P, P, PACK], BF16) for b in range(TILES)]
-        neg_bf = [sbuf(f"neg_bf{o}", [P, P, PACK], BF16) for o in range(PASSES)]
-        neg_codes = [sbuf(f"neg_codes{o}", [P, P], U32) for o in range(PASSES)]
-        neg_plane = [sbuf(f"neg_plane{o}", [P, P], U8) for o in range(PASSES)]
+        c_bf = [sbuf(f"c_bf{o}", [P, N, PACK], BF16) for o in range(PASSES)]
+        neg_cast = sbuf("neg_cast", [P, PASSES * P, PACK], BF16)
+        neg_all = sbuf("neg_all", [P, PASSES * P], U32)
+        neg_scales = sbuf("neg_scales", [P, PASSES * P], U8)
+        neg_bf = [neg_cast[:, o * P : (o + 1) * P, :] for o in range(PASSES)]
+        neg_codes = [neg_all[:, o * P : (o + 1) * P] for o in range(PASSES)]
+        neg_plane = [neg_scales[:, o * P : (o + 1) * P] for o in range(PASSES)]
         c_codes = [sbuf(f"c_codes{o}", [P, N], U32) for o in range(PASSES)]
         c_plane = [sbuf(f"c_plane{o}", [P, N], U8) for o in range(PASSES)]
         HALF = S // 2
@@ -130,10 +132,13 @@ def tile_picked_yrus_burg_p_kernel(tc, x_words, x_scales, cT, area, qm, cur, off
 
         for s in range(2):
             gather_words(s, 0)
-        nc.scalar.copy(*weave(c_bf[0][:], c_raw[0][:]))
-        nc.scalar.activation(neg_bf[0][:], c_bf[0][:, P:N, :], ACT.Copy, scale=-1.0)
-        quantise(c_codes[0][:], c_plane[0][:], c_bf[0][:])
-        quantise(neg_codes[0][:], neg_plane[0][:], neg_bf[0][:])
+        for o in range(PASSES):
+            nc.scalar.copy(*weave(c_bf[o][:], c_raw[o][:]))
+        for o in range(PASSES):
+            nc.scalar.activation(neg_bf[o], c_bf[o][:, P:N, :], ACT.Copy, scale=-1.0)
+        for o in range(PASSES):
+            quantise(c_codes[o][:], c_plane[o][:], c_bf[o][:])
+        quantise(neg_all[:], neg_scales[:], neg_cast[:])
         q_raw = sbuf("q_raw", [P, PACK, R], F32, tag="word_win0")
         nc.sync.dma_start(q_raw[:], qm.rearrange("(p j) r -> p j r", j=PACK))
         area_sb = sbuf("area_sb", [P, PACK], F32, tag="c_bf0")
@@ -141,26 +146,21 @@ def tile_picked_yrus_burg_p_kernel(tc, x_words, x_scales, cT, area, qm, cur, off
 
         for s in range(2):
             products(s, 0)
-        cur_sb = sbuf("cur_sb", [P, R // P, N], F32, tag="x_codes000")
+        cur_sb = sbuf("cur_sb", [P, R // P, N], F32, tag="picked")
         nc.sync.dma_start(cur_sb[:], cur.rearrange("(a p) m -> p a m", p=P))
-        nc.scalar.copy(*weave(c_last[0][:, 0:64, :], c_raw[1][:, :, 0:64]))
-        nc.gpsimd.tensor_scalar(c_last[0][:, 64:P, :], c_raw[1][:, :, 64:P].rearrange("p j r -> p r j"), 1.0, 0.0, ALU.mult, ALU.add)
-        nc.scalar.copy(*weave(c_last[1][:], c_raw[1][:, :, P:N]))
-        nc.scalar.activation(neg_bf[1][:], c_last[1][:], ACT.Copy, scale=-1.0)
-        held = sbuf("x_codes_held", [P, S + HALF], U32, tag="c_raw0")
+        held = sbuf("x_codes_held", [P, 2 * S], U32, tag="c_bf1")
         x_tiles[0, 1, 0] = held[:, 0:S]
         x_tiles[1, 1, 0] = held[:, S : S + HALF]
+        x_tiles[1, 1, HALF] = held[:, S + HALF : 2 * S]
         gather_words(0, 1)
-        gather_words(1, 1, halves[0])
-        quantise(c_codes[1][:, 0:P], c_plane[1][:, 0:P], c_last[0][:])
-        x_tiles[1, 1, HALF] = sbuf("x_codes11last", [P, HALF], U32, tag="c_last0")
-        gather_words(1, 1, halves[1])
-        quantise(c_codes[1][:, P:N], c_plane[1][:, P:N], c_last[1][:])
         for span in halves:
-            for s in range(2):
-                product(s, 1, 0, span)
+            gather_words(1, 1, span)
+        for span in halves:
+            product(0, 1, 0, span)
         product(0, 1, 1, whole[0])
-        product(1, 1, 1, halves[0])
+        for b in range(TILES):
+            product(1, 1, b, halves[0])
+        product(1, 1, 0, halves[1])
 
         def by_slot(bank):
             return bank[:].rearrange("p (q j) -> p j q", j=PACK)
@@ -202,8 +202,7 @@ def tile_picked_yrus_burg_p_kernel(tc, x_words, x_scales, cT, area, qm, cur, off
                 for j in range(PACK):
                     nc.tensor.matmul(flux[b][:, j, :], term[:, j, :], ident[:], start=(n, j) == (0, 0), stop=(n, j) == (1, PACK - 1), is_transpose=True)
 
-        quantise(neg_codes[1][:], neg_plane[1][:], neg_bf[1][:])
-        q_bf = [sbuf("q_bf0", [P, P, PACK], BF16, tag="neg_bf1")]
+        q_bf = [sbuf("q_bf0", [P, P, PACK], BF16, tag="neg_cast")]
         nc.gpsimd.tensor_scalar(q_bf[0][:], q_raw[:, :, 0:P].rearrange("p j r -> p r j"), 1.0, 0.0, ALU.mult, ALU.add)
         jump(0, halves[0])
         crest(0, halves[0])
@@ -230,7 +229,7 @@ def tile_picked_yrus_burg_p_kernel(tc, x_words, x_scales, cT, area, qm, cur, off
         crest(1, halves[0])
         nc.scalar.activation(part(drop_abs[1], last), by_slot(last_drop), ACT.Abs, scale=0.25)
         crest(1, halves[1])
-        q_bf.append(sbuf("q_bf1", [P, P, PACK], BF16, tag="neg_codes1"))
+        q_bf.append(sbuf("q_bf1", [P, P, PACK], BF16, tag="neg_all"))
         nc.scalar.copy(*weave(q_bf[1][:], q_raw[:, :, P:R]))
         signed_square(nc.vector, 0, halves[1])
         turn(0)

@@ -39,7 +39,8 @@ def tile_picked_yrus_burg_p_kernel(tc, x_words, x_scales, cT, area, qm, cur, off
         lists = [keep.tile([P, S // 16], U16, name=f"list{s}") for s in range(2)]
 
         ROWS = PASSES * 16
-        scale_win = sbuf("scale_win", [P, T], U8)
+        lap = ctx.enter_context(tc.tile_pool(name="lap", bufs=1))
+        scale_win = lap.tile([P, T], U8, name="scale_win", align_bytes=64, offset=2 * T)
         nc.vector.memset(scale_win[2 * ROWS : P, :].bitcast(I32), 0)
         nc.gpsimd.memset(scale_win[ROWS : 2 * ROWS, :].bitcast(I32), 0)
         x_plane = [sbuf(f"x_plane{o}", [P, 2 * S], U8) for o in range(PASSES)]
@@ -59,6 +60,9 @@ def tile_picked_yrus_burg_p_kernel(tc, x_words, x_scales, cT, area, qm, cur, off
         load_words(0)
         for o in range(PASSES):
             nc.sync.dma_start(c_raw[o][:], c_rows[o])
+        word_win.append(lap.tile([P, T], U32, name="word_win1", align_bytes=64, offset=0))
+        last_words = x_words[1].rearrange("p n t -> p (n t)").bitcast(I32)
+        nc.sync.dma_start(word_win[1][:, 0 : T // 2].bitcast(I32), last_words[:, 0 : T // 2])
         picked = sbuf("picked", [P, 2 * S], U8)
         for s in range(2):
             nc.vector.tensor_copy(picked[:, s * S : (s + 1) * S], scale_win[:].indirect(lists[s][:]))
@@ -68,8 +72,7 @@ def tile_picked_yrus_burg_p_kernel(tc, x_words, x_scales, cT, area, qm, cur, off
                 nc.sync.dma_start(x_plane[o][32 * quad : 32 * quad + 4, :].bitcast(I32), picked[16 * o + 4 * quad : 16 * o + 4 * quad + 4, :].bitcast(I32))
 
         relay(0)
-        word_win.append(sbuf("word_win1", [P, T], U32, tag="scale_win"))
-        load_words(1)
+        nc.sync.dma_start(word_win[1][:, T // 2 : T].bitcast(I32), last_words[:, T // 2 : T])
         relay(1)
         ident = sbuf("ident", [P, P], F32)
         make_identity(nc, ident[:])
@@ -134,11 +137,11 @@ def tile_picked_yrus_burg_p_kernel(tc, x_words, x_scales, cT, area, qm, cur, off
             gather_words(s, 0)
         for o in range(PASSES):
             nc.scalar.copy(*weave(c_bf[o][:], c_raw[o][:]))
-        for o in range(PASSES):
-            nc.scalar.activation(neg_bf[o], c_bf[o][:, P:N, :], ACT.Copy, scale=-1.0)
+        nc.gpsimd.tensor_scalar(neg_bf[0], c_bf[0][:, P:N, :], -1.0, 0.0, ALU.mult, ALU.add)
+        nc.scalar.activation(neg_bf[1], c_bf[1][:, P:N, :], ACT.Copy, scale=-1.0)
         for o in range(PASSES):
             quantise(c_codes[o][:], c_plane[o][:], c_bf[o][:])
-        quantise(neg_all[:], neg_scales[:], neg_cast[:])
+            quantise(neg_codes[o], neg_plane[o], neg_bf[o])
         q_raw = sbuf("q_raw", [P, PACK, R], F32, tag="word_win0")
         nc.sync.dma_start(q_raw[:], qm.rearrange("(p j) r -> p j r", j=PACK))
         area_sb = sbuf("area_sb", [P, PACK], F32, tag="c_bf0")
@@ -148,7 +151,7 @@ def tile_picked_yrus_burg_p_kernel(tc, x_words, x_scales, cT, area, qm, cur, off
             products(s, 0)
         cur_sb = sbuf("cur_sb", [P, R // P, N], F32, tag="picked")
         nc.sync.dma_start(cur_sb[:], cur.rearrange("(a p) m -> p a m", p=P))
-        held = sbuf("x_codes_held", [P, 2 * S], U32, tag="c_bf1")
+        held = sbuf("x_codes_held", [P, 2 * S], U32, tag="c_raw1")
         x_tiles[0, 1, 0] = held[:, 0:S]
         x_tiles[1, 1, 0] = held[:, S : S + HALF]
         x_tiles[1, 1, HALF] = held[:, S + HALF : 2 * S]

import math
from contextlib import ExitStack

import concourse.mybir as mybir
from concourse.masks import make_identity

K, T, S, N, R = 1024, 2048, 512, 256, 256
FLOPS = 2 * (2 * K * S * N + S * R * N)

F32 = mybir.dt.float32
BF16 = mybir.dt.bfloat16
I32 = mybir.dt.int32
U32 = mybir.dt.uint32
U16 = mybir.dt.uint16
U8 = mybir.dt.uint8
FP8X4 = mybir.dt.float8_e4m3fn_x4
ALU = mybir.AluOpType
ACT = mybir.ActivationFunctionType

P = 128
PACK = 4
PASSES = K // (P * PACK)
TILES = N // P


def weave(woven, rows):
    return (woven.rearrange("p (c i) j -> p c j i", i=4), rows.rearrange("p j (c i) -> p c j i", i=4))


def tile_picked_yrus_burg_p_kernel(tc, x_words, x_scales, cT, area, qm, cur, offs, right, out):
    nc = tc.nc
    with ExitStack() as ctx:
        keep = ctx.enter_context(tc.tile_pool(name="keep", bufs=1))
        psum = ctx.enter_context(tc.psum_pool(name="psum", bufs=1))

        def sbuf(name, shape, dtype, tag=None):
            return keep.tile(shape, dtype, name=name, tag=tag or name, align_bytes=64)

        lists = [keep.tile([P, S // 16], U16, name=f"list{s}") for s in range(2)]

        ROWS = PASSES * 16
        lap = ctx.enter_context(tc.tile_pool(name="lap", bufs=1))
        scale_win = lap.tile([P, T], U8, name="scale_win", align_bytes=64, offset=2 * T)
        nc.vector.memset(scale_win[2 * ROWS : P, :].bitcast(I32), 0)
        nc.gpsimd.memset(scale_win[ROWS : 2 * ROWS, :].bitcast(I32), 0)
        x_plane = [sbuf(f"x_plane{o}", [P, 2 * S], U8) for o in range(PASSES)]
        for o in range(PASSES):
            nc.gpsimd.memset(x_plane[o][:].bitcast(I32), 0)

        word_win = [sbuf("word_win0", [P, T], U32)]
        c_raw = [sbuf(f"c_raw{o}", [P, PACK, N], F32) for o in range(PASSES)]
        c_rows = cT.rearrange("(o p j) m -> o p j m", o=PASSES, j=PACK)

        def load_words(o):
            nc.sync.dma_start(word_win[o][:].bitcast(I32), x_words[o].rearrange("p n t -> p (n t)").bitcast(I32))

        nc.sync.dma_start(scale_win[0:ROWS, :].bitcast(I32), x_scales.rearrange("o q t -> (o q) t").bitcast(I32))
        nc.sync.dma_start(lists[0][:], offs)
        nc.sync.dma_start(lists[1][:], right)
        load_words(0)
        for o in range(PASSES):
            nc.sync.dma_start(c_raw[o][:], c_rows[o])
        word_win.append(lap.tile([P, T], U32, name="word_win1", align_bytes=64, offset=0))
        last_words = x_words[1].rearrange("p n t -> p (n t)").bitcast(I32)
        nc.sync.dma_start(word_win[1][:, 0 : T // 2].bitcast(I32), last_words[:, 0 : T // 2])
        picked = sbuf("picked", [P, 2 * S], U8)
        for s in range(2):
            nc.vector.tensor_copy(picked[:, s * S : (s + 1) * S], scale_win[:].indirect(lists[s][:]))

        def relay(o):
            for quad in range(4):
                nc.sync.dma_start(x_plane[o][32 * quad : 32 * quad + 4, :].bitcast(I32), picked[16 * o + 4 * quad : 16 * o + 4 * quad + 4, :].bitcast(I32))

        relay(0)
        nc.sync.dma_start(word_win[1][:, T // 2 : T].bitcast(I32), last_words[:, T // 2 : T])
        relay(1)
        ident = sbuf("ident", [P, P], F32)
        make_identity(nc, ident[:])

        c_bf = [sbuf(f"c_bf{o}", [P, N, PACK], BF16) for o in range(PASSES)]
        neg_cast = sbuf("neg_cast", [P, PASSES * P, PACK], BF16)
        neg_all = sbuf("neg_all", [P, PASSES * P], U32)
        neg_scales = sbuf("neg_scales", [P, PASSES * P], U8)
        neg_bf = [neg_cast[:, o * P : (o + 1) * P, :] for o in range(PASSES)]
        neg_codes = [neg_all[:, o * P : (o + 1) * P] for o in range(PASSES)]
        neg_plane = [neg_scales[:, o * P : (o + 1) * P] for o in range(PASSES)]
        c_codes = [sbuf(f"c_codes{o}", [P, N], U32) for o in range(PASSES)]
        c_plane = [sbuf(f"c_plane{o}", [P, N], U8) for o in range(PASSES)]
        HALF = S // 2
        whole = [slice(0, S)]
        halves = [slice(0, HALF), slice(HALF, S)]
        x_tiles = {
            (s, o, span.start): sbuf(f"x_codes{s}{o}{span.start}", [P, span.stop - span.start], U32)
            for s in range(2)
            for o in range(PASSES)
            for span in (halves if (s, o) == (1, 1) else whole)
            if (s, o, span.start) not in ((1, 1, HALF), (0, 1, 0), (1, 1, 0))
        }

        def x_codes(s, o, span):
            return x_tiles[s, o, span.start][:] if (s, o) == (1, 1) else x_tiles[s, o, 0][:, span]

        late = (1, 1, HALF)
        spans = {(s, b): whole if (s, b) == (0, 1) else halves for s in range(2) for b in range(TILES)}
        state = {
            (s, b, span.start): psum.tile([P, span.stop - span.start], F32, name=f"state{s}{b}{span.start}")
            for (s, b), cut in spans.items()
            for span in cut
            if (s, b, span.start) != late
        }

        def quantise(codes, plane, woven):
            nc.vector.quantize_mx(out=codes.bitcast(FP8X4), scales=plane, in_=woven.rearrange("p n j -> p (n j)"))

        def gather_words(s, o, span=whole[0]):
            nc.vector.tensor_copy(x_codes(s, o, span), word_win[o][:].indirect(lists[s][:, span.start // 16 : span.stop // 16]))

        def product(s, o, b, span):
            cols = slice(b * P, (b + 1) * P)
            nc.tensor.matmul_mx(
                out=state[s, b, span.start][:],
                lhsT=c_codes[o][:, cols].bitcast(FP8X4),
                lhsT_scale=c_plane[o][:, cols],
                rhs=x_codes(s, o, span).bitcast(FP8X4),
                rhs_scale=x_plane[o][:, s * S + span.start : s * S + span.stop],
                start=(o == 0),
                stop=(o == PASSES - 1),
            )

        def products(s, o):
            for b in range(TILES):
                for span in spans[s, b]:
                    if (s, b, span.start) != late:
                        product(s, o, b, span)

        for s in range(2):
            gather_words(s, 0)
        for o in range(PASSES):
            nc.scalar.copy(*weave(c_bf[o][:], c_raw[o][:]))
        nc.gpsimd.tensor_scalar(neg_bf[0], c_bf[0][:, P:N, :], -1.0, 0.0, ALU.mult, ALU.add)
        nc.scalar.activation(neg_bf[1], c_bf[1][:, P:N, :], ACT.Copy, scale=-1.0)
        for o in range(PASSES):
            quantise(c_codes[o][:], c_plane[o][:], c_bf[o][:])
            quantise(neg_codes[o], neg_plane[o], neg_bf[o])
        q_raw = sbuf("q_raw", [P, PACK, R], F32, tag="word_win0")
        nc.sync.dma_start(q_raw[:], qm.rearrange("(p j) r -> p j r", j=PACK))
        area_sb = sbuf("area_sb", [P, PACK], F32, tag="c_bf0")
        nc.sync.dma_start(area_sb[:], area.rearrange("(p j) o -> p (j o)", j=PACK))

        for s in range(2):
            products(s, 0)
        cur_sb = sbuf("cur_sb", [P, R // P, N], F32, tag="picked")
        nc.sync.dma_start(cur_sb[:], cur.rearrange("(a p) m -> p a m", p=P))
        held = sbuf("x_codes_held", [P, 2 * S], U32, tag="c_raw1")
        x_tiles[0, 1, 0] = held[:, 0:S]
        x_tiles[1, 1, 0] = held[:, S : S + HALF]
        x_tiles[1, 1, HALF] = held[:, S + HALF : 2 * S]
        gather_words(0, 1)
        for span in halves:
            gather_words(1, 1, span)
        for span in halves:
            product(0, 1, 0, span)
        product(0, 1, 1, whole[0])
        for b in range(TILES):
            product(1, 1, b, halves[0])
        product(1, 1, 0, halves[1])

        def by_slot(bank):
            return bank[:].rearrange("p (q j) -> p j q", j=PACK)

        def part(tile, span):
            return tile[:, :, span.start // PACK : span.stop // PACK]

        shape = [P, PACK, P]
        left = [sbuf(f"left{b}", shape, F32) for b in range(TILES)]
        drop = [sbuf(f"drop{b}", shape, F32) for b in range(TILES)]
        drop_abs = [sbuf(f"drop_abs{b}", shape, F32) for b in range(TILES)]
        term_a = [sbuf(f"term_a{b}", shape, F32) for b in range(TILES)]
        term_b = [sbuf(f"term_b{b}", shape, F32) for b in range(TILES)]
        for span in halves:
            nc.scalar.copy(part(left[0], span), by_slot(state[0, 0, span.start]))
        for span in halves:
            nc.scalar.copy(part(left[1], span), part(by_slot(state[0, 1, 0]), span))
        flux = [psum.tile(shape, F32, name=f"flux{b}") for b in range(TILES)]
        fa_bf = [sbuf(f"fa_bf{b}", [P, P, PACK], BF16) for b in range(TILES)]
        fa_codes = [sbuf(f"fa_codes{b}", [P, P], U32, tag=None if b else "term_b1") for b in range(TILES)]
        fa_plane = [sbuf(f"fa_plane{b}", [P, P], U8) for b in range(TILES)]
        area_wide = area_sb[:].unsqueeze(1).to_broadcast([P, P, PACK])

        peak = [sbuf(f"peak{b}", shape, F32, tag=f"peak{b}") for b in range(TILES)]

        def jump(b, span):
            nc.vector.tensor_tensor(part(drop[b], span), part(left[b], span), by_slot(state[1, b, span.start]), ALU.subtract)
            nc.scalar.activation(part(drop_abs[b], span), part(drop[b], span), ACT.Abs, scale=0.25)

        def crest(b, span):
            nc.vector.scalar_tensor_tensor(part(peak[b], span), by_slot(state[1, b, span.start]), -1.0, part(left[b], span), ALU.mult, ALU.max)
            nc.scalar.activation(part(term_a[b], span), part(peak[b], span), ACT.Square, scale=math.sqrt(0.5))

        def signed_square(engine, b, span):
            engine.tensor_tensor(part(term_b[b], span), part(drop_abs[b], span), part(drop[b], span), ALU.mult)

        def turn(b):
            for n, term in enumerate((term_a[b], term_b[b])):
                for j in range(PACK):
                    nc.tensor.matmul(flux[b][:, j, :], term[:, j, :], ident[:], start=(n, j) == (0, 0), stop=(n, j) == (1, PACK - 1), is_transpose=True)

        q_bf = [sbuf("q_bf0", [P, P, PACK], BF16, tag="neg_cast")]
        nc.gpsimd.tensor_scalar(q_bf[0][:], q_raw[:, :, 0:P].rearrange("p j r -> p r j"), 1.0, 0.0, ALU.mult, ALU.add)
        jump(0, halves[0])
        crest(0, halves[0])
        state[late] = psum.tile([P, HALF], F32, name="state_late", tag="state100")
        for o in range(PASSES):
            product(1, o, 1, halves[1])
        jump(0, halves[1])
        crest(0, halves[1])
        signed_square(nc.gpsimd, 0, halves[0])
        last = halves[1]
        last_drop = psum.tile([P, HALF], F32, name="last_drop", tag="state10256")
        for s in range(2):
            for o in range(PASSES):
                nc.tensor.matmul_mx(
                    out=last_drop[:],
                    lhsT=(neg_codes[o][:] if s else c_codes[o][:, P:N]).bitcast(FP8X4),
                    lhsT_scale=neg_plane[o][:] if s else c_plane[o][:, P:N],
                    rhs=x_codes(s, o, last).bitcast(FP8X4),
                    rhs_scale=x_plane[o][:, s * S + last.start : s * S + last.stop],
                    start=(s, o) == (0, 0),
                    stop=(s, o) == (1, PASSES - 1),
                )
        jump(1, halves[0])
        crest(1, halves[0])
        nc.scalar.activation(part(drop_abs[1], last), by_slot(last_drop), ACT.Abs, scale=0.25)
        crest(1, halves[1])
        q_bf.append(sbuf("q_bf1", [P, P, PACK], BF16, tag="neg_all"))
        nc.scalar.copy(*weave(q_bf[1][:], q_raw[:, :, P:R]))
        signed_square(nc.vector, 0, halves[1])
        turn(0)
        signed_square(nc.vector, 1, halves[0])
        q_codes = [sbuf("q_codes0", [P, P], U32, tag="left1")]
        q_plane = [sbuf(f"q_plane{a}", [P, P], U8) for a in range(R // P)]
        quantise(q_codes[0][:], q_plane[0][:], q_bf[0][:])
        nc.vector.tensor_tensor(part(term_b[1], last), part(drop_abs[1], last), by_slot(last_drop), ALU.mult)
        turn(1)
        q_codes.append(sbuf("q_codes1", [P, P], U32, tag="term_a1"))
        for b in range(TILES):
            nc.vector.tensor_tensor(fa_bf[b][:], flux[b][:].rearrange("p j m -> p m j"), area_wide, ALU.mult)
            if b == 0:
                quantise(q_codes[1][:], q_plane[1][:], q_bf[1][:])
        for b in range(TILES):
            quantise(fa_codes[b][:], fa_plane[b][:], fa_bf[b][:])
        out_rows = out.rearrange("(a p) m -> p a m", p=P)
        for b in range(TILES):
            cols = slice(b * P, (b + 1) * P)
            acc = psum.tile([P, R // P, P], F32, name=f"acc{b}", tag=f"state0{b}0")
            for a in range(R // P):
                nc.tensor.matmul_mx(
                    out=acc[:, a, :],
                    lhsT=q_codes[a][:].bitcast(FP8X4),
                    lhsT_scale=q_plane[a][:],
                    rhs=fa_codes[b][:].bitcast(FP8X4),
                    rhs_scale=fa_plane[b][:],
                    start=True,
                    stop=True,
                )
            res = sbuf(f"res{b}", [P, R // P, P], F32)
            nc.vector.scalar_tensor_tensor(res[:], acc[:], -0.5, cur_sb[:, :, cols], ALU.mult, ALU.add)
            queue = nc.sync if b == 0 else nc.scalar
            queue.dma_start(out_rows[:, :, cols], res[:])
